import numpy as np
import ml_dtypes


def mxq(x, axis, fmt="e4m3"):
    dtype, down = {"e4m3": (ml_dtypes.float8_e4m3fn, 7), "e5m2": (ml_dtypes.float8_e5m2, 14)}[fmt]
    v = np.moveaxis(np.asarray(x, np.float32).astype(ml_dtypes.bfloat16).astype(np.float64), axis, -1)
    blocks = v.reshape(v.shape[:-1] + (-1, 32))
    amax = np.abs(blocks).max(-1, keepdims=True)
    byte = np.maximum(np.where(amax > 0, np.frexp(amax)[1] - 1 + 127, 0) - down, 1)
    scale = np.exp2(byte - 127.0)
    codes = (blocks / scale).astype(np.float32).astype(dtype).astype(np.float64)
    return np.moveaxis((codes * scale).reshape(v.shape), -1, axis)


WIDE = False


def mx_kscale(k):
    if not WIDE:
        return np.ones(k)
    levels = np.array([10, -10, 5, -5, 0])
    if k % 512:
        return np.exp2(np.random.permutation(np.resize(levels, k // 32))).repeat(32)
    a = np.empty((k // 512, 16))
    for p in range(k // 512):
        a[p, :8] = np.random.permutation(np.resize(levels, 8))
        for g in range(8):
            far = levels[np.abs(levels - a[p, g]) >= 10]
            a[p, g + 8] = far[np.random.randint(len(far))]
    return np.exp2(a.ravel()).repeat(32)


BF16 = ml_dtypes.bfloat16


def bf(x):
    return np.asarray(x, np.float32).astype(BF16)


def f64(x):
    return np.asarray(x).astype(np.float64)


E2M1 = np.array([0.0, 0.5, 1.0, 1.5, 2.0, 3.0, 4.0, 6.0, -0.0, -0.5, -1.0, -1.5, -2.0, -3.0, -4.0, -6.0])


def pack_weight(w, fmt):
    k, n = w.shape
    w = f64(bf(w)).reshape(k // 32, 32, n)
    amax = np.abs(w).max(1)
    if fmt == "e4m3":
        byte = np.frexp(amax)[1] - 1 + 127 - 7
    else:
        mant, ex = np.frexp(amax / 6.0)
        byte = np.where(mant > 0.5, ex, ex - 1) + 127
    byte = np.clip(np.where(amax > 0, byte, 1), 1, 254)
    scaled = (w * np.exp2(127.0 - byte)[:, None, :]).reshape(k, n).astype(np.float32)
    by_word = np.ascontiguousarray(scaled.reshape(k // 512, 128, 4, n).transpose(0, 1, 3, 2))
    if fmt == "e4m3":
        words = by_word.astype(ml_dtypes.float8_e4m3fn).view(np.uint8)
    else:
        c = by_word.astype(ml_dtypes.float4_e2m1fn).view(np.uint8) & 0xF
        words = c[..., 0::2] | (c[..., 1::2] << 4)
    return np.ascontiguousarray(words), np.ascontiguousarray(byte.astype(np.uint8).reshape(k // 512, 16, n))


def unpack_weight(words, scales, fmt):
    g, p, n, _ = words.shape
    if fmt == "e4m3":
        vals = np.ascontiguousarray(words).view(ml_dtypes.float8_e4m3fn).astype(np.float64)
    else:
        nib = np.empty((g, p, n, 4), np.uint8)
        nib[..., 0::2] = words & 0xF
        nib[..., 1::2] = words >> 4
        vals = E2M1[nib]
    vals = vals * np.repeat(np.exp2(scales.astype(np.float64) - 127.0), 8, axis=1)[..., None]
    return vals.transpose(0, 1, 3, 2).reshape(g * 512, n)
def pack4(w):
    words, scales = pack_weight(w, "e2m1")
    return words.reshape(words.shape[0], 128, -1), scales


def unpack4(words, scales):
    return unpack_weight(words.reshape(words.shape[0], 128, -1, 2), scales, "e2m1")


def planes(Y):
    n, m = Y.shape
    b = f64(bf(Y)).reshape(n // 32, 32, m)
    amax = np.abs(b).max(1)
    byte = np.clip(np.where(amax > 0, np.frexp(amax)[1] - 1 + 127 - 7, 1), 1, 254)
    codes = (b * np.exp2(127.0 - byte)[:, None, :]).reshape(n, m).astype(np.float32).astype(ml_dtypes.float8_e4m3fn).view(np.uint8)
    words = codes.reshape(n // 512, 128, 4, m).transpose(0, 1, 3, 2)
    return np.ascontiguousarray(words), np.ascontiguousarray(byte.astype(np.uint8).reshape(n // 512, 16, m))


G, P, N = 1536, 1024, 1024

def setup_inputs():
    rn = np.random.standard_normal
    s = mx_kscale(P)
    t = mx_kscale(G)
    C = rn((P, N)) * s[:, None]
    T = rn((P, G)) / np.sqrt(P) / s[:, None] / t[None, :]
    B = rn((G, P)) / np.sqrt(P) / s[None, :]
    c_words, c_scales = pack_weight(C, "e4m3")
    t_words, t_scales = pack4(T)
    return {
        "c_words": c_words, "c_scales": c_scales,
        "t_words": t_words, "t_scales": t_scales,
        "basis": bf(B),
        "v": bf(rn(G) / t),
        "w": bf(np.exp(0.3 * rn(G)) / np.sqrt(G) * t),
        "a": bf(0.5 * rn((N, N))),
        "d": bf(np.exp(0.8 * rn(N))),
    }

def reference(c_words, c_scales, t_words, t_scales, basis, v, w, a, d):
    C = unpack_weight(c_words, c_scales, "e4m3")
    T = unpack4(t_words, t_scales)
    Bq = mxq(f64(basis), 1, "e4m3")
    psi = Bq @ C
    kin = T.T @ C
    hpsi = kin + f64(v)[:, None] * psi
    left = f64(w)[:, None] * psi
    leftq = mxq(left, 0, "e4m3")
    hq = mxq(hpsi, 0, "e4m3")
    R = leftq.T @ hq
    y = f64(d)[:, None] * (R + f64(a))
    Y = y.reshape(N, N)
    words, scales = planes(Y)
    return y, words, scales

@@ -1,0 +1,489 @@
+from contextlib import ExitStack
+
+import concourse.mybir as mybir
+from concourse.masks import make_identity
+
+G, K, N = 1536, 1024, 1024
+FLOPS = 2 * G * K * N * 2 + 2 * G * N * N
+
+F32 = mybir.dt.float32
+BF16 = mybir.dt.bfloat16
+U32 = mybir.dt.uint32
+I32 = mybir.dt.int32
+U8 = mybir.dt.uint8
+FP8X4 = mybir.dt.float8_e4m3fn_x4
+FP4X4 = mybir.dt.float4_e2m1fn_x4
+COPY = mybir.ActivationFunctionType.Copy
+ADD = mybir.AluOpType.add
+MULT = mybir.AluOpType.mult
+
+P = 128
+PACK = 4
+PASS = P * PACK
+KG = K // PASS
+GG = G // PASS
+NG = N // PASS
+CW = 128
+NC = N // CW
+LF_FIRST = True
+SLABS = [(0, 256), (256, 256), (512, 256), (768, 128), (896, 128)]
+
+
+def tile_weighted_rayleigh_matrix_k4_kernel(
+    tc, c_words, c_scales, t_words, t_scales, basis, v, w, a, d, out_0, out_1, out_2
+):
+    nc = tc.nc
+
+    with ExitStack() as ctx:
+        keep = ctx.enter_context(tc.tile_pool(name="keep", bufs=1))
+        stage = ctx.enter_context(tc.tile_pool(name="stage", bufs=3))
+        psum = ctx.enter_context(tc.psum_pool(name="psum", bufs=8))
+        ctx.enter_context(tc.manual_schedule())
+
+        def kept(name, shape, dtype):
+            return keep.tile(shape, dtype, name=name, align_bytes=64)
+
+        def staged(tag, shape, dtype, bufs):
+            return stage.tile(shape, dtype, name=tag, tag=tag, bufs=bufs, align_bytes=64)
+
+        def new_bank(shape):
+            return psum.tile(shape, F32, name="bank", tag="bank")
+
+        ident = kept("ident", [P, P], F32)
+        c_codes = kept("c_codes", [P, KG, N], U32)
+        c_plane = kept("c_plane", [P, KG, N], U8)
+        t_raw = kept("t_raw", [P, KG, 2 * G], U8)
+        t_codes = kept("t_codes", [P, KG, 2 * G], U8)
+        t_plane_raw = kept("t_plane_raw", [P, KG, G], U8)
+        t_plane = kept("t_plane", [P, KG, G], U8)
+        b_codes = kept("b_codes", [P, GG, KG, PASS], U32)
+        b_plane = kept("b_plane", [P, GG, KG, PASS], U8)
+        l_codes = kept("l_codes", [P, GG, N], U32)
+        l_plane = kept("l_plane", [P, GG, N], U8)
+        h_codes = kept("h_codes", [P, GG, N], U32)
+        h_plane = kept("h_plane", [P, GG, N], U8)
+        y_codes = kept("y_codes", [P, NG, N], U32)
+        y_plane = kept("y_plane", [P, NG, N], U8)
+        vpsi = kept("vpsi", [P, GG, NC, PACK, CW], F32)
+        vw_rows = kept("vw_rows", [P, PASS], BF16)
+        vw_sorted = kept("vw_sorted", [P, PACK, P], F32)
+        vw = kept("vw", [P, 2 * GG, PACK], F32)
+        d_raw = kept("d_raw", [P, NG, PACK], BF16)
+        d_col = kept("d_col", [P, NG, PACK], F32)
+
+        rows_in = {}
+        b_bf = {}
+        l_bf = {}
+        h_bf = {}
+        y_bf = {}
+        y_f32 = {}
+        da = {}
+        banks = {}
+
+        def load_basis(j, kg, i0, ni):
+            if j not in rows_in:
+                rows_in[j] = staged("rows", [P, PACK, K], BF16, 3)
+            src = basis[PASS * j + P * i0 : PASS * j + P * (i0 + ni), PASS * kg : PASS * (kg + 1)]
+            nc.sync.dma_start(
+                out=rows_in[j][:, i0 : i0 + ni, PASS * kg : PASS * (kg + 1)],
+                in_=src.rearrange("(i p) k -> p i k", p=P),
+            )
+
+        def load_c(q):
+            src = c_words.rearrange("g p n t -> p g (n t)")[:, :, 1024 * q : 1024 * (q + 1)]
+            nc.sync.dma_start(out=c_codes[:, :, 256 * q : 256 * (q + 1)].bitcast(I32), in_=src.bitcast(I32))
+
+        def load_t(j):
+            src = t_words.rearrange("g p b -> p g b")[:, :, 1024 * j : 1024 * (j + 1)]
+            nc.sync.dma_start(out=t_raw[:, :, 1024 * j : 1024 * (j + 1)].bitcast(I32), in_=src.bitcast(I32))
+
+        def load_a(h):
+            rows_in["a", h] = staged("rows", [P, PACK, N], BF16, 3)
+            nc.sync.dma_start(
+                out=rows_in["a", h][:],
+                in_=a[PASS * h : PASS * (h + 1), :].rearrange("(p t) m -> p t m", t=PACK),
+            )
+
+        def load_plane(queue, plane, scales):
+            for q in range(4):
+                queue.dma_start(
+                    out=plane[32 * q : 32 * q + 4, :, :].bitcast(I32),
+                    in_=scales[:, 4 * q : 4 * q + 4, :].rearrange("g r n -> r g n").bitcast(I32),
+                )
+
+        def turn_basis(j, kg, ip):
+            bank = new_bank([P, 2, 2, P])
+            for i in range(2):
+                words = rows_in[j][:, 2 * ip + i, :].bitcast(F32)
+                for u in range(2):
+                    nc.tensor.transpose(bank[:, u, i, :], words[:, 256 * kg + u : 256 * (kg + 1) : 2], ident[:])
+            banks["b", j, kg, ip] = bank
+
+        def copy_basis(j, kg, ip):
+            if j not in b_bf:
+                b_bf[j] = staged("b_bf", [P, KG, PASS * PACK], BF16, 2)
+            dst = b_bf[j][:, kg, :].bitcast(F32).rearrange("p (t c r u) -> p c t r u", t=PACK, r=8, u=2)
+            nc.scalar.copy(
+                out=dst[:, 8 * ip : 8 * ip + 8],
+                in_=banks.pop(("b", j, kg, ip))[:].rearrange("p u i (q t r) -> p (i q) t r u", t=PACK, r=8),
+            )
+
+        def quantize(codes, plane, values):
+            nc.vector.quantize_mx(out=codes.bitcast(FP8X4), scales=plane, in_=values)
+
+        def quant_basis(j, kg, c0, cn):
+            quantize(
+                b_codes[:, j, kg, c0 : c0 + cn],
+                b_plane[:, j, kg, c0 : c0 + cn],
+                b_bf[j][:, kg, PACK * c0 : PACK * (c0 + cn)],
+            )
+
+        def sort_t(j):
+            for kg in range(KG):
+                cols = slice(1024 * j, 1024 * (j + 1))
+                nc.vector.tensor_copy(
+                    out=t_codes[:, kg, cols].bitcast(I32).rearrange("p (t q x) -> p t q x", t=PACK, x=4),
+                    in_=t_raw[:, kg, cols].bitcast(I32).rearrange("p (q t x) -> p t q x", t=PACK, x=4),
+                )
+                cols = slice(PASS * j, PASS * (j + 1))
+                nc.vector.tensor_copy(
+                    out=t_plane[:, kg, cols].bitcast(I32).rearrange("p (t q x) -> p t q x", t=PACK, x=2),
+                    in_=t_plane_raw[:, kg, cols].bitcast(I32).rearrange("p (q t x) -> p t q x", t=PACK, x=2),
+                )
+
+        def stage_one(key, c, stationary):
+            bank = new_bank([P, PACK, CW])
+            cols = slice(CW * c, CW * (c + 1))
+            for t in range(PACK):
+                for kg in range(KG):
+                    codes, plane = stationary(t, kg)
+                    nc.tensor.matmul_mx(
+                        out=bank[:, t, :],
+                        lhsT=codes,
+                        lhsT_scale=plane,
+                        rhs=c_codes[:, kg, cols].bitcast(FP8X4),
+                        rhs_scale=c_plane[:, kg, cols],
+                        start=(kg == 0),
+                        stop=(kg == KG - 1),
+                    )
+            banks[key] = bank
+
+        def psi(j, c):
+            stage_one(
+                ("psi", j, c),
+                c,
+                lambda t, kg: (
+                    b_codes[:, j, kg, P * t : P * (t + 1)].bitcast(FP8X4),
+                    b_plane[:, j, kg, P * t : P * (t + 1)],
+                ),
+            )
+
+        def kin(j, c):
+            stage_one(
+                ("kin", j, c),
+                c,
+                lambda t, kg: (
+                    t_codes[:, kg, 2 * (PASS * j + P * t) : 2 * (PASS * j + P * (t + 1))].bitcast(FP4X4),
+                    t_plane[:, kg, PASS * j + P * t : PASS * j + P * (t + 1)],
+                ),
+            )
+
+        def scale_v(j, c):
+            for t in range(PACK):
+                nc.scalar.activation(
+                    out=vpsi[:, j, c, t, :], in_=banks["psi", j, c][:, t, :], func=COPY, scale=vw[:, j, t : t + 1]
+                )
+
+        def left(j, c):
+            h, cc = divmod(c, 4)
+            if cc == 0:
+                l_bf[j, h] = staged("l_bf", [P, PACK, P, PACK], BF16, 2)
+            weight = vw[:, GG + j, :].rearrange("p (a b t) -> p a b t", a=1, b=1)
+            nc.vector.tensor_tensor(
+                out=l_bf[j, h][:, :, 32 * cc : 32 * (cc + 1), :],
+                in0=banks.pop(("psi", j, c))[:].rearrange("p t (m s) -> p s m t", s=PACK),
+                in1=weight.to_broadcast([P, PACK, 32, PACK]),
+                op=MULT,
+            )
+
+        def quant_left(j, h):
+            cols = slice(PASS * h, PASS * (h + 1))
+            quantize(l_codes[:, j, cols], l_plane[:, j, cols], l_bf.pop((j, h))[:].rearrange("p s m t -> p (s m t)"))
+
+        def slab_of(c):
+            return [s for s, (c0, cn) in enumerate(SLABS) if c0 <= CW * c < c0 + cn][0]
+
+        def hpsi(j, c):
+            s = slab_of(c)
+            c0, cn = SLABS[s]
+            if (j, s) not in h_bf:
+                h_bf[j, s] = staged("h_bf", [P, cn, PACK], BF16, 4)
+            off = CW * c - c0
+            nc.vector.tensor_tensor(
+                out=h_bf[j, s][:, off : off + CW, :].rearrange("p (c i) t -> p c t i", i=2),
+                in0=banks.pop(("kin", j, c))[:].rearrange("p t (c i) -> p c t i", i=2),
+                in1=vpsi[:, j, c].rearrange("p t (c i) -> p c t i", i=2),
+                op=ADD,
+            )
+
+        def quant_hpsi(j, s):
+            c0, cn = SLABS[s]
+            cols = slice(c0, c0 + cn)
+            quantize(h_codes[:, j, cols], h_plane[:, j, cols], h_bf.pop((j, s))[:].rearrange("p c t -> p (c t)"))
+
+        def scale_a(s, h):
+            c0, cn = 256 * s, 256
+            da[s, h] = staged("da", [P, PACK, cn], F32, 3)
+            for t in range(PACK):
+                nc.scalar.activation(
+                    out=da[s, h][:, t, :],
+                    in_=rows_in["a", h][:, t, c0 : c0 + cn],
+                    func=COPY,
+                    scale=d_col[:, h, t : t + 1],
+                )
+
+        def slots(s, b):
+            per_bank = 4 if s == 3 else 2
+            return range(per_bank * b, per_bank * (b + 1))
+
+        def rayleigh(s, h, b):
+            c0, cn = SLABS[s]
+            cols = slice(c0, c0 + cn)
+            bank = new_bank([P, len(slots(s, b)), cn])
+            for i, t in enumerate(slots(s, b)):
+                rows = slice(PASS * h + P * t, PASS * h + P * (t + 1))
+                for j in range(GG):
+                    nc.tensor.matmul_mx(
+                        out=bank[:, i, :],
+                        lhsT=l_codes[:, j, rows].bitcast(FP8X4),
+                        lhsT_scale=l_plane[:, j, rows],
+                        rhs=h_codes[:, j, cols].bitcast(FP8X4),
+                        rhs_scale=h_plane[:, j, cols],
+                        start=(j == 0),
+                        stop=(j == GG - 1),
+                    )
+            banks["r", s, h, b] = bank
+
+        def finish_y(s, h, b):
+            c0, cn = SLABS[s]
+            if b == 0:
+                y_f32[s, h] = staged("y_f32", [P, PACK, cn], F32, 4)
+            bank = banks.pop(("r", s, h, b))
+            for i, t in enumerate(slots(s, b)):
+                nc.vector.scalar_tensor_tensor(
+                    out=y_f32[s, h][:, t, :],
+                    in0=bank[:, i, :],
+                    scalar=d_col[:, h, t : t + 1],
+                    in1=da[c0 // 256, h][:, t, c0 % 256 : c0 % 256 + cn],
+                    op0=MULT,
+                    op1=ADD,
+                )
+
+        def store_y(s, h):
+            c0, cn = SLABS[s]
+            dst = out_0[PASS * h : PASS * (h + 1), c0 : c0 + cn]
+            nc.sync.dma_start(out=dst.rearrange("(p t) m -> p t m", t=PACK), in_=y_f32[s, h][:])
+
+        def round_y(s, h, on_vector):
+            c0, cn = SLABS[s]
+            y_bf[s, h] = staged("y_bf", [P, cn, PACK], BF16, 3)
+            dst = y_bf[s, h][:].rearrange("p (c i) t -> p c t i", i=2)
+            src = y_f32[s, h][:].rearrange("p t (c i) -> p c t i", i=2)
+            if on_vector:
+                nc.vector.tensor_copy(out=dst, in_=src)
+            else:
+                nc.scalar.copy(out=dst, in_=src)
+
+        def quant_y(s, h):
+            c0, cn = SLABS[s]
+            cols = slice(c0, c0 + cn)
+            quantize(y_codes[:, h, cols], y_plane[:, h, cols], y_bf.pop((s, h))[:].rearrange("p c t -> p (c t)"))
+
+        def store_codes(s, h):
+            c0, cn = SLABS[s]
+            dst = out_1[h].rearrange("p m t -> p (m t)")[:, PACK * c0 : PACK * (c0 + cn)]
+            nc.sync.dma_start(out=dst.bitcast(I32), in_=y_codes[:, h, c0 : c0 + cn].bitcast(I32))
+
+        def store_scales(c0, cn, queues):
+            for q in range(4):
+                queues[q % len(queues)].dma_start(
+                    out=out_2[:, 4 * q : 4 * q + 4, c0 : c0 + cn].rearrange("g r n -> r g n").bitcast(I32),
+                    in_=y_plane[32 * q : 32 * q + 4, :, c0 : c0 + cn].bitcast(I32),
+                )
+
+        nc.vector.memset(vw_rows[:], 0.0)
+        nc.vector.memset(c_plane[:].bitcast(I32), 0)
+        nc.vector.memset(t_plane_raw[:].bitcast(I32), 0)
+        make_identity(nc, ident[:])
+        nc.scalar.dma_start(out=d_raw[:], in_=d.rearrange("(h p t) -> p h t", p=P, t=PACK))
+        nc.gpsimd.dma_start(out=vw_rows[0:GG, :], in_=v.rearrange("(j g) -> j g", j=GG))
+        nc.gpsimd.dma_start(out=vw_rows[GG : 2 * GG, :], in_=w.rearrange("(j g) -> j g", j=GG))
+        load_plane(nc.gpsimd, t_plane_raw, t_scales)
+        for kg in range(KG):
+            for ip in range(2):
+                load_basis(0, kg, 2 * ip, 2)
+        load_c(0)
+        load_plane(nc.sync, c_plane, c_scales)
+        load_t(0)
+        load_c(1)
+        load_basis(1, 0, 0, 4)
+        load_c(2)
+        load_basis(1, 1, 0, 4)
+        load_c(3)
+        load_t(1)
+        load_t(2)
+        load_basis(2, 0, 0, 4)
+        load_basis(2, 1, 0, 4)
+        load_a(0)
+        load_a(1)
+
+        nc.scalar.activation(out=d_col[:], in_=d_raw[:], func=COPY)
+        nc.vector.tensor_copy(
+            out=vw_sorted[:].rearrange("p t (q r) -> p t q r", r=8),
+            in_=vw_rows[:].rearrange("p (q t r) -> p t q r", t=PACK, r=8),
+        )
+        for ip in range(2):
+            turn_basis(0, 0, ip)
+            copy_basis(0, 0, ip)
+        quant_basis(0, 0, 0, PASS)
+        for ip in range(2):
+            turn_basis(0, 1, ip)
+            copy_basis(0, 1, ip)
+        vw_bank = new_bank([P, PACK, P])
+        for t in range(PACK):
+            nc.tensor.transpose(vw_bank[:, t, :], vw_sorted[:, t, :], ident[:])
+        quant_basis(0, 1, 0, 256)
+        quant_basis(0, 1, 256, 256)
+        nc.vector.tensor_copy(out=vw[:], in_=vw_bank[:, :, 0 : 2 * GG].rearrange("p t c -> p c t"))
+        sort_t(0)
+
+        def turn_half(j, kg):
+            for ip in range(2):
+                turn_basis(j, kg, ip)
+            for ip in range(2):
+                copy_basis(j, kg, ip)
+
+        def psi_step(j, c):
+            psi(j, c)
+            if LF_FIRST:
+                bank = banks["psi", j, c]
+                left(j, c)
+                banks["psi", j, c] = bank
+                scale_v(j, c)
+            else:
+                scale_v(j, c)
+                left(j, c)
+
+        def kin_step(j, c):
+            kin(j, c)
+            hpsi(j, c)
+
+        for j in range(GG):
+            more = j + 1 < GG
+            psi_step(j, 0)
+            if j > 0:
+                quant_left(j - 1, 1)
+            psi_step(j, 1)
+            if more:
+                turn_half(j + 1, 0)
+            psi_step(j, 2)
+            psi_step(j, 3)
+            if more:
+                turn_half(j + 1, 1)
+            if more:
+                quant_basis(j + 1, 0, 0, PASS)
+            kin_step(j, 0)
+            psi_step(j, 4)
+            quant_left(j, 0)
+            kin_step(j, 1)
+            if more:
+                quant_basis(j + 1, 1, 0, PASS)
+            psi_step(j, 5)
+            quant_hpsi(j, 0)
+            psi_step(j, 6)
+            if more:
+                sort_t(j + 1)
+            psi_step(j, 7)
+        scale_a(0, 0)
+        scale_a(0, 1)
+
+        pending = []
+        for s in range(3):
+            if s < 2:
+                ks = [(j, 2 * (s + 1) + i) for j in range(GG) for i in range(2)]
+            else:
+                ks = [(j, 6 + i) for i in range(2) for j in range(GG)]
+
+            def quant_step(n):
+                j, c = ks[n]
+                if s == 2 or c % 2 == 1:
+                    quant_hpsi(j, slab_of(c))
+
+            kin_step(*ks[0])
+            if s == 0:
+                quant_left(GG - 1, 1)
+            kin_step(*ks[1])
+            quant_step(0)
+            for item in pending:
+                quant_y(*item)
+                store_codes(*item)
+            pending = []
+            rayleigh(s, 0, 0)
+            finish_y(s, 0, 0)
+            quant_step(1)
+            kin_step(*ks[2])
+            rayleigh(s, 0, 1)
+            finish_y(s, 0, 1)
+            store_y(s, 0)
+            round_y(s, 0, False)
+            scale_a(s + 1, 0)
+            quant_step(2)
+            kin_step(*ks[3])
+            rayleigh(s, 1, 0)
+            finish_y(s, 1, 0)
+            quant_step(3)
+            kin_step(*ks[4])
+            rayleigh(s, 1, 1)
+            finish_y(s, 1, 1)
+            store_y(s, 1)
+            round_y(s, 1, False)
+            scale_a(s + 1, 1)
+            quant_step(4)
+            kin_step(*ks[5])
+            quant_y(s, 0)
+            store_codes(s, 0)
+            quant_step(5)
+            pending = [(s, 1)]
+
+        rayleigh(3, 0, 0)
+        finish_y(3, 0, 0)
+        store_y(3, 0)
+        round_y(3, 0, False)
+        quant_y(2, 1)
+        store_codes(2, 1)
+        store_scales(0, 768, [nc.sync])
+        rayleigh(3, 1, 0)
+        finish_y(3, 1, 0)
+        store_y(3, 1)
+        round_y(3, 1, False)
+        rayleigh(4, 0, 0)
+        finish_y(4, 0, 0)
+        rayleigh(4, 0, 1)
+        finish_y(4, 0, 1)
+        store_y(4, 0)
+        round_y(4, 0, False)
+        quant_y(3, 0)
+        store_codes(3, 0)
+        rayleigh(4, 1, 0)
+        finish_y(4, 1, 0)
+        quant_y(3, 1)
+        store_codes(3, 1)
+        rayleigh(4, 1, 1)
+        finish_y(4, 1, 1)
+        store_y(4, 1)
+        quant_y(4, 0)
+        store_codes(4, 0)
+        round_y(4, 1, True)
+        quant_y(4, 1)
+        store_codes(4, 1)
+        store_scales(768, 256, [nc.scalar, nc.sync])

@@ -25,8 +25,8 @@ GG = G // PASS
 NG = N // PASS
 CW = 128
 NC = N // CW
-LF_FIRST = True
-SLABS = [(0, 256), (256, 256), (512, 256), (768, 128), (896, 128)]
+SLABS = [(0, 512), (512, 256), (768, 128), (896, 128)]
+HQ = [(0, 256), (256, 256), (512, 256), (768, 128), (896, 128)]
 
 
 def tile_weighted_rayleigh_matrix_k4_kernel(
@@ -38,7 +38,7 @@ def tile_weighted_rayleigh_matrix_k4_kernel(
         keep = ctx.enter_context(tc.tile_pool(name="keep", bufs=1))
         stage = ctx.enter_context(tc.tile_pool(name="stage", bufs=3))
         psum = ctx.enter_context(tc.psum_pool(name="psum", bufs=8))
-        ctx.enter_context(tc.manual_schedule())
+        ctx.enter_context(tc.manual_schedule(engines={mybir.EngineType.PE, mybir.EngineType.SP}))
 
         def kept(name, shape, dtype):
             return keep.tile(shape, dtype, name=name, align_bytes=64)
@@ -52,10 +52,10 @@ def tile_weighted_rayleigh_matrix_k4_kernel(
         ident = kept("ident", [P, P], F32)
         c_codes = kept("c_codes", [P, KG, N], U32)
         c_plane = kept("c_plane", [P, KG, N], U8)
-        t_raw = kept("t_raw", [P, KG, 2 * G], U8)
-        t_codes = kept("t_codes", [P, KG, 2 * G], U8)
+        t_raw = kept("t_raw", [P, GG, KG, 2 * PASS], U8)
+        t_codes = kept("t_codes", [P, GG, PACK, KG, 2 * P], U8)
         t_plane_raw = kept("t_plane_raw", [P, KG, G], U8)
-        t_plane = kept("t_plane", [P, KG, G], U8)
+        t_plane = kept("t_plane", [P, PACK, KG, GG, P], U8)
         b_codes = kept("b_codes", [P, GG, KG, PASS], U32)
         b_plane = kept("b_plane", [P, GG, KG, PASS], U8)
         l_codes = kept("l_codes", [P, GG, N], U32)
@@ -64,7 +64,6 @@ def tile_weighted_rayleigh_matrix_k4_kernel(
         h_plane = kept("h_plane", [P, GG, N], U8)
         y_codes = kept("y_codes", [P, NG, N], U32)
         y_plane = kept("y_plane", [P, NG, N], U8)
-        vpsi = kept("vpsi", [P, GG, NC, PACK, CW], F32)
         vw_rows = kept("vw_rows", [P, PASS], BF16)
         vw_sorted = kept("vw_sorted", [P, PACK, P], F32)
         vw = kept("vw", [P, 2 * GG, PACK], F32)
@@ -74,6 +73,8 @@ def tile_weighted_rayleigh_matrix_k4_kernel(
         rows_in = {}
         b_bf = {}
         l_bf = {}
+        l_rows = {}
+        vpsi = {}
         h_bf = {}
         y_bf = {}
         y_f32 = {}
@@ -95,7 +96,7 @@ def tile_weighted_rayleigh_matrix_k4_kernel(
 
         def load_t(j):
             src = t_words.rearrange("g p b -> p g b")[:, :, 1024 * j : 1024 * (j + 1)]
-            nc.sync.dma_start(out=t_raw[:, :, 1024 * j : 1024 * (j + 1)].bitcast(I32), in_=src.bitcast(I32))
+            nc.sync.dma_start(out=t_raw[:, j].bitcast(I32), in_=src.bitcast(I32))
 
         def load_a(h):
             rows_in["a", h] = staged("rows", [P, PACK, N], BF16, 3)
@@ -121,7 +122,7 @@ def tile_weighted_rayleigh_matrix_k4_kernel(
 
         def copy_basis(j, kg, ip):
             if j not in b_bf:
-                b_bf[j] = staged("b_bf", [P, KG, PASS * PACK], BF16, 2)
+                b_bf[j] = staged("big", [P, KG, PASS * PACK], BF16, 5)
             dst = b_bf[j][:, kg, :].bitcast(F32).rearrange("p (t c r u) -> p c t r u", t=PACK, r=8, u=2)
             nc.scalar.copy(
                 out=dst[:, 8 * ip : 8 * ip + 8],
@@ -139,17 +140,16 @@ def tile_weighted_rayleigh_matrix_k4_kernel(
             )
 
         def sort_t(j):
-            for kg in range(KG):
-                cols = slice(1024 * j, 1024 * (j + 1))
-                nc.vector.tensor_copy(
-                    out=t_codes[:, kg, cols].bitcast(I32).rearrange("p (t q x) -> p t q x", t=PACK, x=4),
-                    in_=t_raw[:, kg, cols].bitcast(I32).rearrange("p (q t x) -> p t q x", t=PACK, x=4),
-                )
-                cols = slice(PASS * j, PASS * (j + 1))
-                nc.vector.tensor_copy(
-                    out=t_plane[:, kg, cols].bitcast(I32).rearrange("p (t q x) -> p t q x", t=PACK, x=2),
-                    in_=t_plane_raw[:, kg, cols].bitcast(I32).rearrange("p (q t x) -> p t q x", t=PACK, x=2),
-                )
+            nc.vector.tensor_copy(
+                out=t_codes[:, j].bitcast(I32).rearrange("p t g (q x) -> p t g q x", x=4),
+                in_=t_raw[:, j].bitcast(I32).rearrange("p g (q t x) -> p t g q x", t=PACK, x=4),
+            )
+
+        def sort_t_plane():
+            nc.vector.tensor_copy(
+                out=t_plane[:].bitcast(I32).rearrange("p t g j (q x) -> p t g (j q) x", x=2),
+                in_=t_plane_raw[:].bitcast(I32).rearrange("p g (b t x) -> p t g b x", t=PACK, x=2),
+            )
 
         def stage_one(key, c, stationary):
             bank = new_bank([P, PACK, CW])
@@ -183,21 +183,26 @@ def tile_weighted_rayleigh_matrix_k4_kernel(
                 ("kin", j, c),
                 c,
                 lambda t, kg: (
-                    t_codes[:, kg, 2 * (PASS * j + P * t) : 2 * (PASS * j + P * (t + 1))].bitcast(FP4X4),
-                    t_plane[:, kg, PASS * j + P * t : PASS * j + P * (t + 1)],
+                    t_codes[:, j, t, kg, :].bitcast(FP4X4),
+                    t_plane[:, t, kg, j, :],
                 ),
             )
 
         def scale_v(j, c):
+            if (j, c // 4) not in vpsi:
+                vpsi[j, c // 4] = staged("vpsi", [P, PACK, PASS], F32, 5)
             for t in range(PACK):
                 nc.scalar.activation(
-                    out=vpsi[:, j, c, t, :], in_=banks["psi", j, c][:, t, :], func=COPY, scale=vw[:, j, t : t + 1]
+                    out=vpsi[j, c // 4][:, t, CW * (c % 4) : CW * (c % 4 + 1)],
+                    in_=banks["psi", j, c][:, t, :],
+                    func=COPY,
+                    scale=vw[:, j, t : t + 1],
                 )
 
         def left(j, c):
             h, cc = divmod(c, 4)
             if cc == 0:
-                l_bf[j, h] = staged("l_bf", [P, PACK, P, PACK], BF16, 2)
+                l_bf[j, h] = staged("l_bf", [P, PACK, P, PACK], BF16, 3)
             weight = vw[:, GG + j, :].rearrange("p (a b t) -> p a b t", a=1, b=1)
             nc.vector.tensor_tensor(
                 out=l_bf[j, h][:, :, 32 * cc : 32 * (cc + 1), :],
@@ -206,34 +211,65 @@ def tile_weighted_rayleigh_matrix_k4_kernel(
                 op=MULT,
             )
 
+        def wide_step(j, h, t):
+            bank = new_bank([P, PASS])
+            cols = slice(PASS * h, PASS * (h + 1))
+            for kg in range(KG):
+                nc.tensor.matmul_mx(
+                    out=bank[:],
+                    lhsT=b_codes[:, j, kg, P * t : P * (t + 1)].bitcast(FP8X4),
+                    lhsT_scale=b_plane[:, j, kg, P * t : P * (t + 1)],
+                    rhs=c_codes[:, kg, cols].bitcast(FP8X4),
+                    rhs_scale=c_plane[:, kg, cols],
+                    start=(kg == 0),
+                    stop=(kg == KG - 1),
+                )
+            if t == 0:
+                vpsi[j, h] = staged("vpsi", [P, PACK, PASS], F32, 5)
+                l_rows[j, h] = staged("big", [P, PACK, PASS], BF16, 5)
+            nc.scalar.activation(
+                out=l_rows[j, h][:, t, :].rearrange("p (s m) -> p s m", s=PACK),
+                in_=bank[:].rearrange("p (m s) -> p s m", s=PACK),
+                func=COPY,
+                scale=vw[:, GG + j, t : t + 1],
+            )
+            nc.scalar.activation(out=vpsi[j, h][:, t, :], in_=bank[:], func=COPY, scale=vw[:, j, t : t + 1])
+
+        def weave_left(j, h):
+            l_bf[j, h] = staged("l_bf", [P, PACK, P, PACK], BF16, 3)
+            nc.vector.tensor_copy(
+                out=l_bf[j, h][:].rearrange("p s (c i) t -> p (s c) t i", i=4),
+                in_=l_rows.pop((j, h))[:].rearrange("p t (c i) -> p c t i", i=4),
+            )
+
         def quant_left(j, h):
             cols = slice(PASS * h, PASS * (h + 1))
             quantize(l_codes[:, j, cols], l_plane[:, j, cols], l_bf.pop((j, h))[:].rearrange("p s m t -> p (s m t)"))
 
         def slab_of(c):
-            return [s for s, (c0, cn) in enumerate(SLABS) if c0 <= CW * c < c0 + cn][0]
+            return [s for s, (c0, cn) in enumerate(HQ) if c0 <= CW * c < c0 + cn][0]
 
         def hpsi(j, c):
             s = slab_of(c)
-            c0, cn = SLABS[s]
+            c0, cn = HQ[s]
             if (j, s) not in h_bf:
                 h_bf[j, s] = staged("h_bf", [P, cn, PACK], BF16, 4)
             off = CW * c - c0
             nc.vector.tensor_tensor(
                 out=h_bf[j, s][:, off : off + CW, :].rearrange("p (c i) t -> p c t i", i=2),
                 in0=banks.pop(("kin", j, c))[:].rearrange("p t (c i) -> p c t i", i=2),
-                in1=vpsi[:, j, c].rearrange("p t (c i) -> p c t i", i=2),
+                in1=vpsi[j, c // 4][:, :, CW * (c % 4) : CW * (c % 4 + 1)].rearrange("p t (c i) -> p c t i", i=2),
                 op=ADD,
             )
 
         def quant_hpsi(j, s):
-            c0, cn = SLABS[s]
+            c0, cn = HQ[s]
             cols = slice(c0, c0 + cn)
             quantize(h_codes[:, j, cols], h_plane[:, j, cols], h_bf.pop((j, s))[:].rearrange("p c t -> p (c t)"))
 
         def scale_a(s, h):
-            c0, cn = 256 * s, 256
-            da[s, h] = staged("da", [P, PACK, cn], F32, 3)
+            c0, cn = PASS * s, PASS
+            da[s, h] = staged("big", [P, PACK, cn], F32, 5)
             for t in range(PACK):
                 nc.scalar.activation(
                     out=da[s, h][:, t, :],
@@ -243,7 +279,7 @@ def tile_weighted_rayleigh_matrix_k4_kernel(
                 )
 
         def slots(s, b):
-            per_bank = 4 if s == 3 else 2
+            per_bank = [1, 2, 4, 2][s]
             return range(per_bank * b, per_bank * (b + 1))
 
         def rayleigh(s, h, b):
@@ -267,14 +303,14 @@ def tile_weighted_rayleigh_matrix_k4_kernel(
         def finish_y(s, h, b):
             c0, cn = SLABS[s]
             if b == 0:
-                y_f32[s, h] = staged("y_f32", [P, PACK, cn], F32, 4)
+                y_f32[s, h] = staged(["rows", "big"][h] if cn == PASS else "y_f32", [P, PACK, cn], F32, [3, 5][h] if cn == PASS else 5)
             bank = banks.pop(("r", s, h, b))
             for i, t in enumerate(slots(s, b)):
                 nc.vector.scalar_tensor_tensor(
                     out=y_f32[s, h][:, t, :],
                     in0=bank[:, i, :],
                     scalar=d_col[:, h, t : t + 1],
-                    in1=da[c0 // 256, h][:, t, c0 % 256 : c0 % 256 + cn],
+                    in1=da[c0 // PASS, h][:, t, c0 % PASS : c0 % PASS + cn],
                     op0=MULT,
                     op1=ADD,
                 )
@@ -284,9 +320,14 @@ def tile_weighted_rayleigh_matrix_k4_kernel(
             dst = out_0[PASS * h : PASS * (h + 1), c0 : c0 + cn]
             nc.sync.dma_start(out=dst.rearrange("(p t) m -> p t m", t=PACK), in_=y_f32[s, h][:])
 
+        def store_row(s, h, t):
+            c0, cn = SLABS[s]
+            dst = out_0[PASS * h : PASS * (h + 1), c0 : c0 + cn].rearrange("(p t) m -> p t m", t=PACK)
+            nc.sync.dma_start(out=dst[:, t, :], in_=y_f32[s, h][:, t, :])
+
         def round_y(s, h, on_vector):
             c0, cn = SLABS[s]
-            y_bf[s, h] = staged("y_bf", [P, cn, PACK], BF16, 3)
+            y_bf[s, h] = staged("l_bf", [P, cn, PACK], BF16, 3)
             dst = y_bf[s, h][:].rearrange("p (c i) t -> p c t i", i=2)
             src = y_f32[s, h][:].rearrange("p t (c i) -> p c t i", i=2)
             if on_vector:
@@ -299,10 +340,9 @@ def tile_weighted_rayleigh_matrix_k4_kernel(
             cols = slice(c0, c0 + cn)
             quantize(y_codes[:, h, cols], y_plane[:, h, cols], y_bf.pop((s, h))[:].rearrange("p c t -> p (c t)"))
 
-        def store_codes(s, h):
-            c0, cn = SLABS[s]
-            dst = out_1[h].rearrange("p m t -> p (m t)")[:, PACK * c0 : PACK * (c0 + cn)]
-            nc.sync.dma_start(out=dst.bitcast(I32), in_=y_codes[:, h, c0 : c0 + cn].bitcast(I32))
+        def store_codes(c0, cn):
+            dst = out_1.rearrange("h p m t -> p h (m t)")[:, :, PACK * c0 : PACK * (c0 + cn)]
+            nc.sync.dma_start(out=dst.bitcast(I32), in_=y_codes[:, :, c0 : c0 + cn].bitcast(I32))
 
         def store_scales(c0, cn, queues):
             for q in range(4):
@@ -316,20 +356,20 @@ def tile_weighted_rayleigh_matrix_k4_kernel(
         nc.vector.memset(t_plane_raw[:].bitcast(I32), 0)
         make_identity(nc, ident[:])
         nc.scalar.dma_start(out=d_raw[:], in_=d.rearrange("(h p t) -> p h t", p=P, t=PACK))
-        nc.gpsimd.dma_start(out=vw_rows[0:GG, :], in_=v.rearrange("(j g) -> j g", j=GG))
-        nc.gpsimd.dma_start(out=vw_rows[GG : 2 * GG, :], in_=w.rearrange("(j g) -> j g", j=GG))
-        load_plane(nc.gpsimd, t_plane_raw, t_scales)
+        nc.scalar.dma_start(out=vw_rows[0:GG, :], in_=v.rearrange("(j g) -> j g", j=GG))
+        nc.scalar.dma_start(out=vw_rows[GG : 2 * GG, :], in_=w.rearrange("(j g) -> j g", j=GG))
         for kg in range(KG):
             for ip in range(2):
                 load_basis(0, kg, 2 * ip, 2)
         load_c(0)
         load_plane(nc.sync, c_plane, c_scales)
-        load_t(0)
-        load_c(1)
         load_basis(1, 0, 0, 4)
+        load_c(1)
         load_c(2)
-        load_basis(1, 1, 0, 4)
         load_c(3)
+        load_plane(nc.sync, t_plane_raw, t_scales)
+        load_t(0)
+        load_basis(1, 1, 0, 4)
         load_t(1)
         load_t(2)
         load_basis(2, 0, 0, 4)
@@ -355,7 +395,7 @@ def tile_weighted_rayleigh_matrix_k4_kernel(
         quant_basis(0, 1, 0, 256)
         quant_basis(0, 1, 256, 256)
         nc.vector.tensor_copy(out=vw[:], in_=vw_bank[:, :, 0 : 2 * GG].rearrange("p t c -> p c t"))
-        sort_t(0)
+        sort_t_plane()
 
         def turn_half(j, kg):
             for ip in range(2):
@@ -365,125 +405,164 @@ def tile_weighted_rayleigh_matrix_k4_kernel(
 
         def psi_step(j, c):
             psi(j, c)
-            if LF_FIRST:
-                bank = banks["psi", j, c]
-                left(j, c)
-                banks["psi", j, c] = bank
-                scale_v(j, c)
-            else:
-                scale_v(j, c)
-                left(j, c)
+            bank = banks["psi", j, c]
+            left(j, c)
+            banks["psi", j, c] = bank
+            scale_v(j, c)
 
         def kin_step(j, c):
             kin(j, c)
             hpsi(j, c)
 
-        for j in range(GG):
-            more = j + 1 < GG
-            psi_step(j, 0)
-            if j > 0:
-                quant_left(j - 1, 1)
-            psi_step(j, 1)
-            if more:
-                turn_half(j + 1, 0)
-            psi_step(j, 2)
-            psi_step(j, 3)
-            if more:
-                turn_half(j + 1, 1)
-            if more:
-                quant_basis(j + 1, 0, 0, PASS)
-            kin_step(j, 0)
-            psi_step(j, 4)
-            quant_left(j, 0)
-            kin_step(j, 1)
-            if more:
-                quant_basis(j + 1, 1, 0, PASS)
-            psi_step(j, 5)
-            quant_hpsi(j, 0)
-            psi_step(j, 6)
-            if more:
-                sort_t(j + 1)
-            psi_step(j, 7)
+        sort_t(0)
+        psi_step(0, 0)
+        psi_step(0, 1)
+        turn_half(1, 0)
+        wide_step(0, 1, 0)
+        psi_step(0, 2)
+        psi_step(0, 3)
+        turn_half(1, 1)
+        kin_step(0, 0)
+        kin_step(0, 1)
+        quant_basis(1, 0, 0, PASS)
+        quant_left(0, 0)
+        wide_step(0, 1, 1)
+        wide_step(0, 1, 2)
+        wide_step(0, 1, 3)
+        weave_left(0, 1)
+        kin_step(0, 2)
+        quant_basis(1, 1, 0, PASS)
+        quant_left(0, 1)
+        kin_step(0, 3)
+        quant_hpsi(0, 0)
+        quant_hpsi(0, 1)
+        sort_t(1)
+        psi_step(1, 0)
+        psi_step(1, 1)
+        turn_half(2, 0)
+        wide_step(1, 1, 0)
+        psi_step(1, 2)
+        psi_step(1, 3)
+        kin_step(0, 4)
+        kin_step(0, 5)
+        turn_half(2, 1)
+        kin_step(1, 0)
+        kin_step(1, 1)
+        quant_basis(2, 0, 0, PASS)
+        quant_left(1, 0)
+        wide_step(1, 1, 1)
+        wide_step(1, 1, 2)
+        quant_hpsi(0, 2)
+        wide_step(1, 1, 3)
+        weave_left(1, 1)
+        kin_step(1, 2)
+        quant_basis(2, 1, 0, PASS)
+        quant_left(1, 1)
+        kin_step(1, 3)
+        quant_hpsi(1, 0)
+        quant_hpsi(1, 1)
+        sort_t(2)
+        psi_step(2, 0)
+        psi_step(2, 1)
+        wide_step(2, 1, 0)
+        psi_step(2, 2)
+        psi_step(2, 3)
+        kin_step(1, 4)
+        kin_step(1, 5)
+        kin_step(2, 0)
+        kin_step(2, 1)
+        quant_left(2, 0)
+        wide_step(2, 1, 1)
+        wide_step(2, 1, 2)
+        quant_hpsi(1, 2)
+        wide_step(2, 1, 3)
+        weave_left(2, 1)
+        kin_step(2, 2)
+        quant_left(2, 1)
+        kin_step(2, 3)
+        quant_hpsi(2, 0)
+        quant_hpsi(2, 1)
+        kin_step(2, 4)
+        kin_step(2, 5)
+        quant_hpsi(2, 2)
         scale_a(0, 0)
         scale_a(0, 1)
-
-        pending = []
-        for s in range(3):
-            if s < 2:
-                ks = [(j, 2 * (s + 1) + i) for j in range(GG) for i in range(2)]
-            else:
-                ks = [(j, 6 + i) for i in range(2) for j in range(GG)]
-
-            def quant_step(n):
-                j, c = ks[n]
-                if s == 2 or c % 2 == 1:
-                    quant_hpsi(j, slab_of(c))
-
-            kin_step(*ks[0])
-            if s == 0:
-                quant_left(GG - 1, 1)
-            kin_step(*ks[1])
-            quant_step(0)
-            for item in pending:
-                quant_y(*item)
-                store_codes(*item)
-            pending = []
-            rayleigh(s, 0, 0)
-            finish_y(s, 0, 0)
-            quant_step(1)
-            kin_step(*ks[2])
-            rayleigh(s, 0, 1)
-            finish_y(s, 0, 1)
-            store_y(s, 0)
-            round_y(s, 0, False)
-            scale_a(s + 1, 0)
-            quant_step(2)
-            kin_step(*ks[3])
-            rayleigh(s, 1, 0)
-            finish_y(s, 1, 0)
-            quant_step(3)
-            kin_step(*ks[4])
-            rayleigh(s, 1, 1)
-            finish_y(s, 1, 1)
-            store_y(s, 1)
-            round_y(s, 1, False)
-            scale_a(s + 1, 1)
-            quant_step(4)
-            kin_step(*ks[5])
-            quant_y(s, 0)
-            store_codes(s, 0)
-            quant_step(5)
-            pending = [(s, 1)]
-
+        rayleigh(0, 0, 0)
+        finish_y(0, 0, 0)
+        kin_step(0, 6)
+        rayleigh(0, 0, 1)
+        finish_y(0, 0, 1)
+        rayleigh(0, 0, 2)
+        finish_y(0, 0, 2)
+        kin_step(1, 6)
+        rayleigh(0, 0, 3)
+        finish_y(0, 0, 3)
+        store_y(0, 0)
+        round_y(0, 0, False)
+        scale_a(1, 0)
+        scale_a(1, 1)
+        rayleigh(0, 1, 0)
+        finish_y(0, 1, 0)
+        kin_step(2, 6)
+        rayleigh(0, 1, 1)
+        finish_y(0, 1, 1)
+        quant_hpsi(0, 3)
+        quant_hpsi(1, 3)
+        quant_hpsi(2, 3)
+        rayleigh(0, 1, 2)
+        finish_y(0, 1, 2)
+        kin_step(0, 7)
+        rayleigh(0, 1, 3)
+        finish_y(0, 1, 3)
+        store_y(0, 1)
+        round_y(0, 1, False)
+        rayleigh(1, 0, 0)
+        finish_y(1, 0, 0)
+        kin_step(1, 7)
+        rayleigh(1, 0, 1)
+        finish_y(1, 0, 1)
+        store_y(1, 0)
+        round_y(1, 0, False)
+        quant_y(0, 0)
+        kin_step(2, 7)
+        rayleigh(1, 1, 0)
+        finish_y(1, 1, 0)
+        quant_hpsi(0, 4)
+        quant_hpsi(1, 4)
+        quant_hpsi(2, 4)
+        rayleigh(1, 1, 1)
+        finish_y(1, 1, 1)
+        store_y(1, 1)
+        round_y(1, 1, False)
+        quant_y(0, 1)
+        store_codes(0, 512)
+        rayleigh(2, 0, 0)
+        finish_y(2, 0, 0)
+        store_y(2, 0)
+        round_y(2, 0, False)
+        quant_y(1, 0)
+        rayleigh(2, 1, 0)
+        finish_y(2, 1, 0)
+        store_y(2, 1)
+        round_y(2, 1, False)
+        quant_y(1, 1)
+        store_codes(512, 256)
+        store_scales(0, 768, [nc.sync])
         rayleigh(3, 0, 0)
         finish_y(3, 0, 0)
+        rayleigh(3, 0, 1)
+        finish_y(3, 0, 1)
         store_y(3, 0)
         round_y(3, 0, False)
-        quant_y(2, 1)
-        store_codes(2, 1)
-        store_scales(0, 768, [nc.sync])
+        quant_y(2, 0)
         rayleigh(3, 1, 0)
         finish_y(3, 1, 0)
+        rayleigh(3, 1, 1)
+        finish_y(3, 1, 1)
         store_y(3, 1)
-        round_y(3, 1, False)
-        rayleigh(4, 0, 0)
-        finish_y(4, 0, 0)
-        rayleigh(4, 0, 1)
-        finish_y(4, 0, 1)
-        store_y(4, 0)
-        round_y(4, 0, False)
+        quant_y(2, 1)
+        round_y(3, 1, True)
         quant_y(3, 0)
-        store_codes(3, 0)
-        rayleigh(4, 1, 0)
-        finish_y(4, 1, 0)
         quant_y(3, 1)
-        store_codes(3, 1)
-        rayleigh(4, 1, 1)
-        finish_y(4, 1, 1)
-        store_y(4, 1)
-        quant_y(4, 0)
-        store_codes(4, 0)
-        round_y(4, 1, True)
-        quant_y(4, 1)
-        store_codes(4, 1)
+        store_codes(768, 256)
         store_scales(768, 256, [nc.scalar, nc.sync])

@@ -25,8 +25,8 @@ GG = G // PASS
 NG = N // PASS
 CW = 128
 NC = N // CW
-SLABS = [(0, 512), (512, 256), (768, 128), (896, 128)]
-HQ = [(0, 256), (256, 256), (512, 256), (768, 128), (896, 128)]
+SLABS = [(0, 512), (512, 256), (768, 128), (896, 128), (768, 256)]
+HQ = [(0, 256), (256, 256), (512, 256), (768, 256)]
 
 
 def tile_weighted_rayleigh_matrix_k4_kernel(
@@ -38,7 +38,7 @@ def tile_weighted_rayleigh_matrix_k4_kernel(
         keep = ctx.enter_context(tc.tile_pool(name="keep", bufs=1))
         stage = ctx.enter_context(tc.tile_pool(name="stage", bufs=3))
         psum = ctx.enter_context(tc.psum_pool(name="psum", bufs=8))
-        ctx.enter_context(tc.manual_schedule(engines={mybir.EngineType.PE, mybir.EngineType.SP}))
+        ctx.enter_context(tc.manual_schedule())
 
         def kept(name, shape, dtype):
             return keep.tile(shape, dtype, name=name, align_bytes=64)
@@ -201,12 +201,12 @@ def tile_weighted_rayleigh_matrix_k4_kernel(
 
         def left(j, c):
             h, cc = divmod(c, 4)
-            if cc == 0:
+            if (j, h) not in l_bf:
                 l_bf[j, h] = staged("l_bf", [P, PACK, P, PACK], BF16, 3)
             weight = vw[:, GG + j, :].rearrange("p (a b t) -> p a b t", a=1, b=1)
             nc.vector.tensor_tensor(
                 out=l_bf[j, h][:, :, 32 * cc : 32 * (cc + 1), :],
-                in0=banks.pop(("psi", j, c))[:].rearrange("p t (m s) -> p s m t", s=PACK),
+                in0=banks["psi", j, c][:].rearrange("p t (m s) -> p s m t", s=PACK),
                 in1=weight.to_broadcast([P, PACK, 32, PACK]),
                 op=MULT,
             )
@@ -224,7 +224,11 @@ def tile_weighted_rayleigh_matrix_k4_kernel(
                     start=(kg == 0),
                     stop=(kg == KG - 1),
                 )
-            if t == 0:
+            banks["wide", j, h, t] = bank
+
+        def wide_act(j, h, t):
+            bank = banks.pop(("wide", j, h, t))
+            if (j, h) not in vpsi:
                 vpsi[j, h] = staged("vpsi", [P, PACK, PASS], F32, 5)
                 l_rows[j, h] = staged("big", [P, PACK, PASS], BF16, 5)
             nc.scalar.activation(
@@ -279,7 +283,7 @@ def tile_weighted_rayleigh_matrix_k4_kernel(
                 )
 
         def slots(s, b):
-            per_bank = [1, 2, 4, 2][s]
+            per_bank = [1, 2, 4, 2, 2][s]
             return range(per_bank * b, per_bank * (b + 1))
 
         def rayleigh(s, h, b):
@@ -302,7 +306,7 @@ def tile_weighted_rayleigh_matrix_k4_kernel(
 
         def finish_y(s, h, b):
             c0, cn = SLABS[s]
-            if b == 0:
+            if (s, h) not in y_f32:
                 y_f32[s, h] = staged(["rows", "big"][h] if cn == PASS else "y_f32", [P, PACK, cn], F32, [3, 5][h] if cn == PASS else 5)
             bank = banks.pop(("r", s, h, b))
             for i, t in enumerate(slots(s, b)):
@@ -355,37 +359,36 @@ def tile_weighted_rayleigh_matrix_k4_kernel(
         nc.vector.memset(c_plane[:].bitcast(I32), 0)
         nc.vector.memset(t_plane_raw[:].bitcast(I32), 0)
         make_identity(nc, ident[:])
-        nc.scalar.dma_start(out=d_raw[:], in_=d.rearrange("(h p t) -> p h t", p=P, t=PACK))
-        nc.scalar.dma_start(out=vw_rows[0:GG, :], in_=v.rearrange("(j g) -> j g", j=GG))
-        nc.scalar.dma_start(out=vw_rows[GG : 2 * GG, :], in_=w.rearrange("(j g) -> j g", j=GG))
+        nc.gpsimd.dma_start(out=vw_rows[0:GG, :], in_=v.rearrange("(j g) -> j g", j=GG))
+        nc.gpsimd.dma_start(out=vw_rows[GG : 2 * GG, :], in_=w.rearrange("(j g) -> j g", j=GG))
         for kg in range(KG):
             for ip in range(2):
                 load_basis(0, kg, 2 * ip, 2)
-        load_c(0)
         load_plane(nc.sync, c_plane, c_scales)
+        load_c(0)
         load_basis(1, 0, 0, 4)
-        load_c(1)
         load_c(2)
         load_c(3)
         load_plane(nc.sync, t_plane_raw, t_scales)
         load_t(0)
+        load_c(1)
         load_basis(1, 1, 0, 4)
         load_t(1)
         load_t(2)
         load_basis(2, 0, 0, 4)
         load_basis(2, 1, 0, 4)
+        nc.sync.dma_start(out=d_raw[:], in_=d.rearrange("(h p t) -> p h t", p=P, t=PACK))
         load_a(0)
         load_a(1)
 
-        nc.scalar.activation(out=d_col[:], in_=d_raw[:], func=COPY)
-        nc.vector.tensor_copy(
-            out=vw_sorted[:].rearrange("p t (q r) -> p t q r", r=8),
-            in_=vw_rows[:].rearrange("p (q t r) -> p t q r", t=PACK, r=8),
-        )
         for ip in range(2):
             turn_basis(0, 0, ip)
             copy_basis(0, 0, ip)
         quant_basis(0, 0, 0, PASS)
+        nc.vector.tensor_copy(
+            out=vw_sorted[:].rearrange("p t (q r) -> p t q r", r=8),
+            in_=vw_rows[:].rearrange("p (q t r) -> p t q r", t=PACK, r=8),
+        )
         for ip in range(2):
             turn_basis(0, 1, ip)
             copy_basis(0, 1, ip)
@@ -395,174 +398,233 @@ def tile_weighted_rayleigh_matrix_k4_kernel(
         quant_basis(0, 1, 0, 256)
         quant_basis(0, 1, 256, 256)
         nc.vector.tensor_copy(out=vw[:], in_=vw_bank[:, :, 0 : 2 * GG].rearrange("p t c -> p c t"))
-        sort_t_plane()
+
+        def widen_d(j):
+            nc.scalar.activation(out=d_col[:], in_=d_raw[:], func=COPY)
+
+        def sort_plane(j):
+            sort_t_plane()
 
         def turn_half(j, kg):
             for ip in range(2):
                 turn_basis(j, kg, ip)
+
+        def copy_half(j, kg):
             for ip in range(2):
                 copy_basis(j, kg, ip)
-
-        def psi_step(j, c):
-            psi(j, c)
-            bank = banks["psi", j, c]
-            left(j, c)
-            banks["psi", j, c] = bank
-            scale_v(j, c)
 
         def kin_step(j, c):
             kin(j, c)
             hpsi(j, c)
 
-        sort_t(0)
-        psi_step(0, 0)
-        psi_step(0, 1)
+        psi(0, 0)
         turn_half(1, 0)
+        sort_plane(0)
+        sort_t(0)
+        left(0, 0)
+        copy_half(1, 0)
         wide_step(0, 1, 0)
-        psi_step(0, 2)
-        psi_step(0, 3)
-        turn_half(1, 1)
-        kin_step(0, 0)
-        kin_step(0, 1)
-        quant_basis(1, 0, 0, PASS)
-        quant_left(0, 0)
+        psi(0, 1)
+        wide_act(0, 1, 0)
+        psi(0, 2)
+        scale_v(0, 0)
+        left(0, 1)
+        psi(0, 3)
+        scale_v(0, 1)
+        left(0, 2)
+        scale_v(0, 2)
+        left(0, 3)
+        kin(0, 0)
         wide_step(0, 1, 1)
+        hpsi(0, 0)
+        wide_act(0, 1, 1)
+        kin(0, 1)
+        quant_left(0, 0)
+        turn_half(1, 1)
+        hpsi(0, 1)
+        copy_half(1, 1)
         wide_step(0, 1, 2)
-        wide_step(0, 1, 3)
-        weave_left(0, 1)
-        kin_step(0, 2)
-        quant_basis(1, 1, 0, PASS)
-        quant_left(0, 1)
-        kin_step(0, 3)
+        quant_basis(1, 0, 0, PASS)
+        scale_v(0, 3)
+        kin(0, 2)
         quant_hpsi(0, 0)
+        wide_act(0, 1, 2)
+        kin(0, 3)
+        quant_basis(1, 1, 0, PASS)
+        hpsi(0, 2)
+        wide_step(0, 1, 3)
+        hpsi(0, 3)
+        wide_act(0, 1, 3)
         quant_hpsi(0, 1)
-        sort_t(1)
-        psi_step(1, 0)
-        psi_step(1, 1)
+        weave_left(0, 1)
+        psi(1, 0)
         turn_half(2, 0)
+        sort_t(1)
+        left(1, 0)
+        copy_half(2, 0)
         wide_step(1, 1, 0)
-        psi_step(1, 2)
-        psi_step(1, 3)
-        kin_step(0, 4)
-        kin_step(0, 5)
-        turn_half(2, 1)
-        kin_step(1, 0)
-        kin_step(1, 1)
-        quant_basis(2, 0, 0, PASS)
-        quant_left(1, 0)
+        psi(1, 1)
+        wide_act(1, 1, 0)
+        kin(0, 4)
+        hpsi(0, 4)
+        psi(1, 2)
+        scale_v(1, 0)
+        left(1, 1)
+        psi(1, 3)
+        scale_v(1, 1)
+        left(1, 2)
+        kin(0, 5)
+        scale_v(1, 2)
+        left(1, 3)
+        kin(1, 0)
+        hpsi(0, 5)
         wide_step(1, 1, 1)
+        hpsi(1, 0)
+        wide_act(1, 1, 1)
+        kin(1, 1)
+        quant_left(1, 0)
+        turn_half(2, 1)
+        hpsi(1, 1)
+        copy_half(2, 1)
+        quant_left(0, 1)
         wide_step(1, 1, 2)
-        quant_hpsi(0, 2)
-        wide_step(1, 1, 3)
-        weave_left(1, 1)
-        kin_step(1, 2)
-        quant_basis(2, 1, 0, PASS)
-        quant_left(1, 1)
-        kin_step(1, 3)
+        quant_basis(2, 0, 0, PASS)
+        scale_v(1, 3)
+        kin(1, 2)
         quant_hpsi(1, 0)
+        wide_act(1, 1, 2)
+        kin(1, 3)
+        quant_basis(2, 1, 0, PASS)
+        hpsi(1, 2)
+        wide_step(1, 1, 3)
+        hpsi(1, 3)
+        quant_hpsi(0, 2)
+        wide_act(1, 1, 3)
         quant_hpsi(1, 1)
+        weave_left(1, 1)
+        psi(2, 0)
         sort_t(2)
-        psi_step(2, 0)
-        psi_step(2, 1)
+        left(2, 0)
         wide_step(2, 1, 0)
-        psi_step(2, 2)
-        psi_step(2, 3)
-        kin_step(1, 4)
-        kin_step(1, 5)
-        kin_step(2, 0)
-        kin_step(2, 1)
-        quant_left(2, 0)
+        psi(2, 1)
+        wide_act(2, 1, 0)
+        kin(1, 4)
+        hpsi(1, 4)
+        psi(2, 2)
+        scale_v(2, 0)
+        left(2, 1)
+        psi(2, 3)
+        scale_v(2, 1)
+        left(2, 2)
+        kin(1, 5)
+        scale_v(2, 2)
+        left(2, 3)
+        kin(2, 0)
+        hpsi(1, 5)
         wide_step(2, 1, 1)
+        hpsi(2, 0)
+        wide_act(2, 1, 1)
+        kin(2, 1)
+        quant_left(2, 0)
+        hpsi(2, 1)
+        quant_left(1, 1)
         wide_step(2, 1, 2)
-        quant_hpsi(1, 2)
-        wide_step(2, 1, 3)
-        weave_left(2, 1)
-        kin_step(2, 2)
-        quant_left(2, 1)
-        kin_step(2, 3)
+        scale_v(2, 3)
+        kin(2, 2)
         quant_hpsi(2, 0)
+        wide_act(2, 1, 2)
+        kin(2, 3)
+        hpsi(2, 2)
+        wide_step(2, 1, 3)
+        hpsi(2, 3)
+        quant_hpsi(1, 2)
+        wide_act(2, 1, 3)
         quant_hpsi(2, 1)
-        kin_step(2, 4)
-        kin_step(2, 5)
+        weave_left(2, 1)
+        kin(2, 4)
+        hpsi(2, 4)
+        kin(2, 5)
+        hpsi(2, 5)
+        quant_left(2, 1)
         quant_hpsi(2, 2)
+        widen_d(0)
         scale_a(0, 0)
         scale_a(0, 1)
-        rayleigh(0, 0, 0)
-        finish_y(0, 0, 0)
-        kin_step(0, 6)
-        rayleigh(0, 0, 1)
-        finish_y(0, 0, 1)
-        rayleigh(0, 0, 2)
-        finish_y(0, 0, 2)
-        kin_step(1, 6)
-        rayleigh(0, 0, 3)
-        finish_y(0, 0, 3)
-        store_y(0, 0)
-        round_y(0, 0, False)
         scale_a(1, 0)
         scale_a(1, 1)
-        rayleigh(0, 1, 0)
-        finish_y(0, 1, 0)
-        kin_step(2, 6)
-        rayleigh(0, 1, 1)
-        finish_y(0, 1, 1)
+        kin(0, 6)
+        kin(0, 7)
+        hpsi(0, 6)
+        rayleigh(0, 0, 0)
+        hpsi(0, 7)
+        kin(1, 6)
+        finish_y(0, 0, 0)
+        store_row(0, 0, 0)
+        rayleigh(0, 0, 1)
+        hpsi(1, 6)
         quant_hpsi(0, 3)
+        kin(1, 7)
+        finish_y(0, 0, 1)
+        store_row(0, 0, 1)
+        rayleigh(0, 0, 2)
+        hpsi(1, 7)
+        rayleigh(0, 0, 3)
+        finish_y(0, 0, 2)
+        store_row(0, 0, 2)
         quant_hpsi(1, 3)
-        quant_hpsi(2, 3)
+        kin(2, 6)
+        finish_y(0, 0, 3)
+        store_row(0, 0, 3)
+        round_y(0, 0, False)
+        rayleigh(0, 1, 0)
+        hpsi(2, 6)
+        kin(2, 7)
+        finish_y(0, 1, 0)
+        store_row(0, 1, 0)
+        rayleigh(0, 1, 1)
+        hpsi(2, 7)
         rayleigh(0, 1, 2)
-        finish_y(0, 1, 2)
-        kin_step(0, 7)
+        finish_y(0, 1, 1)
+        store_row(0, 1, 1)
+        quant_hpsi(2, 3)
         rayleigh(0, 1, 3)
-        finish_y(0, 1, 3)
-        store_y(0, 1)
-        round_y(0, 1, False)
+        finish_y(0, 1, 2)
+        store_row(0, 1, 2)
         rayleigh(1, 0, 0)
-        finish_y(1, 0, 0)
-        kin_step(1, 7)
+        finish_y(0, 1, 3)
+        store_row(0, 1, 3)
+        round_y(0, 1, False)
+        quant_y(0, 0)
         rayleigh(1, 0, 1)
+        finish_y(1, 0, 0)
+        rayleigh(1, 1, 0)
         finish_y(1, 0, 1)
         store_y(1, 0)
         round_y(1, 0, False)
-        quant_y(0, 0)
-        kin_step(2, 7)
-        rayleigh(1, 1, 0)
-        finish_y(1, 1, 0)
-        quant_hpsi(0, 4)
-        quant_hpsi(1, 4)
-        quant_hpsi(2, 4)
         rayleigh(1, 1, 1)
+        finish_y(1, 1, 0)
+        quant_y(0, 1)
+        store_codes(0, 512)
+        store_scales(0, 512, [nc.sync])
+        rayleigh(4, 0, 0)
         finish_y(1, 1, 1)
         store_y(1, 1)
         round_y(1, 1, False)
-        quant_y(0, 1)
-        store_codes(0, 512)
-        rayleigh(2, 0, 0)
-        finish_y(2, 0, 0)
-        store_y(2, 0)
-        round_y(2, 0, False)
         quant_y(1, 0)
-        rayleigh(2, 1, 0)
-        finish_y(2, 1, 0)
-        store_y(2, 1)
-        round_y(2, 1, False)
+        rayleigh(4, 0, 1)
+        finish_y(4, 0, 0)
+        rayleigh(4, 1, 0)
+        finish_y(4, 0, 1)
+        store_y(4, 0)
+        round_y(4, 0, False)
         quant_y(1, 1)
         store_codes(512, 256)
-        store_scales(0, 768, [nc.sync])
-        rayleigh(3, 0, 0)
-        finish_y(3, 0, 0)
-        rayleigh(3, 0, 1)
-        finish_y(3, 0, 1)
-        store_y(3, 0)
-        round_y(3, 0, False)
-        quant_y(2, 0)
-        rayleigh(3, 1, 0)
-        finish_y(3, 1, 0)
-        rayleigh(3, 1, 1)
-        finish_y(3, 1, 1)
-        store_y(3, 1)
-        quant_y(2, 1)
-        round_y(3, 1, True)
-        quant_y(3, 0)
-        quant_y(3, 1)
+        rayleigh(4, 1, 1)
+        finish_y(4, 1, 0)
+        finish_y(4, 1, 1)
+        round_y(4, 1, True)
+        store_y(4, 1)
+        quant_y(4, 0)
+        quant_y(4, 1)
         store_codes(768, 256)
-        store_scales(768, 256, [nc.scalar, nc.sync])
+        store_scales(512, 512, [nc.scalar, nc.sync])

@@ -20,13 +20,13 @@ MULT = mybir.AluOpType.mult
 P = 128
 PACK = 4
 PASS = P * PACK
+RUN = 8
 KG = K // PASS
 GG = G // PASS
 NG = N // PASS
-CW = 128
-NC = N // CW
-SLABS = [(0, 512), (512, 256), (768, 128), (896, 128), (768, 256)]
-HQ = [(0, 256), (256, 256), (512, 256), (768, 256)]
+CW = PASS // PACK
+C_PIECE = 256
+SLABS = [(0, 512), (512, 256), (768, 256)]
 
 
 def tile_weighted_rayleigh_matrix_k4_kernel(
@@ -43,8 +43,10 @@ def tile_weighted_rayleigh_matrix_k4_kernel(
         def kept(name, shape, dtype):
             return keep.tile(shape, dtype, name=name, align_bytes=64)
 
-        def staged(tag, shape, dtype, bufs):
-            return stage.tile(shape, dtype, name=tag, tag=tag, bufs=bufs, align_bytes=64)
+        depth = {"rows": 3, "big": 5, "vpsi": 5, "woven": 3, "h_bf": 3, "y_f32": 4}
+
+        def staged(tag, shape, dtype):
+            return stage.tile(shape, dtype, name=tag, tag=tag, bufs=depth[tag], align_bytes=64)
 
         def new_bank(shape):
             return psum.tile(shape, F32, name="bank", tag="bank")
@@ -53,7 +55,7 @@ def tile_weighted_rayleigh_matrix_k4_kernel(
         c_codes = kept("c_codes", [P, KG, N], U32)
         c_plane = kept("c_plane", [P, KG, N], U8)
         t_raw = kept("t_raw", [P, GG, KG, 2 * PASS], U8)
-        t_codes = kept("t_codes", [P, GG, PACK, KG, 2 * P], U8)
+        t_codes = kept("t_codes", [P, PACK, GG, KG, 2 * P], U8)
         t_plane_raw = kept("t_plane_raw", [P, KG, G], U8)
         t_plane = kept("t_plane", [P, PACK, KG, GG, P], U8)
         b_codes = kept("b_codes", [P, GG, KG, PASS], U32)
@@ -70,233 +72,221 @@ def tile_weighted_rayleigh_matrix_k4_kernel(
         d_raw = kept("d_raw", [P, NG, PACK], BF16)
         d_col = kept("d_col", [P, NG, PACK], F32)
 
-        rows_in = {}
-        b_bf = {}
-        l_bf = {}
-        l_rows = {}
-        vpsi = {}
-        h_bf = {}
-        y_bf = {}
-        y_f32 = {}
-        da = {}
-        banks = {}
+        b_rows, a_rows, b_bf, l_rows, l_bf, vpsi = {}, {}, {}, {}, {}, {}
+        h_bf, da, y_f32, y_bf, banks = {}, {}, {}, {}, {}
 
         def load_basis(j, kg, i0, ni):
-            if j not in rows_in:
-                rows_in[j] = staged("rows", [P, PACK, K], BF16, 3)
+            if j not in b_rows:
+                b_rows[j] = staged("rows", [P, PACK, K], BF16)
             src = basis[PASS * j + P * i0 : PASS * j + P * (i0 + ni), PASS * kg : PASS * (kg + 1)]
             nc.sync.dma_start(
-                out=rows_in[j][:, i0 : i0 + ni, PASS * kg : PASS * (kg + 1)],
+                out=b_rows[j][:, i0 : i0 + ni, PASS * kg : PASS * (kg + 1)],
                 in_=src.rearrange("(i p) k -> p i k", p=P),
             )
 
-        def load_c(q):
-            src = c_words.rearrange("g p n t -> p g (n t)")[:, :, 1024 * q : 1024 * (q + 1)]
-            nc.sync.dma_start(out=c_codes[:, :, 256 * q : 256 * (q + 1)].bitcast(I32), in_=src.bitcast(I32))
+        def load_c(n):
+            cols = slice(C_PIECE * n, C_PIECE * (n + 1))
+            src = c_words.rearrange("g p n t -> p g (n t)")[:, :, PACK * cols.start : PACK * cols.stop]
+            nc.sync.dma_start(out=c_codes[:, :, cols].bitcast(I32), in_=src.bitcast(I32))
 
         def load_t(j):
-            src = t_words.rearrange("g p b -> p g b")[:, :, 1024 * j : 1024 * (j + 1)]
+            src = t_words.rearrange("g p b -> p g b")[:, :, 2 * PASS * j : 2 * PASS * (j + 1)]
             nc.sync.dma_start(out=t_raw[:, j].bitcast(I32), in_=src.bitcast(I32))
 
         def load_a(h):
-            rows_in["a", h] = staged("rows", [P, PACK, N], BF16, 3)
+            a_rows[h] = staged("rows", [P, PACK, N], BF16)
             nc.sync.dma_start(
-                out=rows_in["a", h][:],
-                in_=a[PASS * h : PASS * (h + 1), :].rearrange("(p t) m -> p t m", t=PACK),
+                out=a_rows[h][:], in_=a[PASS * h : PASS * (h + 1), :].rearrange("(p t) m -> p t m", t=PACK)
             )
 
-        def load_plane(queue, plane, scales):
-            for q in range(4):
-                queue.dma_start(
-                    out=plane[32 * q : 32 * q + 4, :, :].bitcast(I32),
-                    in_=scales[:, 4 * q : 4 * q + 4, :].rearrange("g r n -> r g n").bitcast(I32),
+        def load_plane(plane, scales):
+            for quad in range(4):
+                nc.sync.dma_start(
+                    out=plane[32 * quad : 32 * quad + 4, :, :].bitcast(I32),
+                    in_=scales[:, 4 * quad : 4 * quad + 4, :].rearrange("g r n -> r g n").bitcast(I32),
                 )
-
-        def turn_basis(j, kg, ip):
-            bank = new_bank([P, 2, 2, P])
-            for i in range(2):
-                words = rows_in[j][:, 2 * ip + i, :].bitcast(F32)
-                for u in range(2):
-                    nc.tensor.transpose(bank[:, u, i, :], words[:, 256 * kg + u : 256 * (kg + 1) : 2], ident[:])
-            banks["b", j, kg, ip] = bank
-
-        def copy_basis(j, kg, ip):
-            if j not in b_bf:
-                b_bf[j] = staged("big", [P, KG, PASS * PACK], BF16, 5)
-            dst = b_bf[j][:, kg, :].bitcast(F32).rearrange("p (t c r u) -> p c t r u", t=PACK, r=8, u=2)
-            nc.scalar.copy(
-                out=dst[:, 8 * ip : 8 * ip + 8],
-                in_=banks.pop(("b", j, kg, ip))[:].rearrange("p u i (q t r) -> p (i q) t r u", t=PACK, r=8),
-            )
 
         def quantize(codes, plane, values):
             nc.vector.quantize_mx(out=codes.bitcast(FP8X4), scales=plane, in_=values)
 
-        def quant_basis(j, kg, c0, cn):
+        def turn_pair(j, kg, pair):
+            bank = new_bank([P, 2, 2, P])
+            for i in range(2):
+                words = b_rows[j][:, 2 * pair + i, :].bitcast(F32)
+                first = kg * PASS // 2
+                for u in range(2):
+                    nc.tensor.transpose(bank[:, u, i, :], words[:, first + u : first + PASS // 2 : 2], ident[:])
+            banks["basis", j, kg, pair] = bank
+
+        def copy_pair(j, kg, pair):
+            if j not in b_bf:
+                b_bf[j] = staged("big", [P, KG, PASS * PACK], BF16)
+            dst = b_bf[j][:, kg, :].bitcast(F32).rearrange("p (t q r u) -> p q t r u", t=PACK, r=RUN, u=2)
+            src = banks.pop(("basis", j, kg, pair))
+            nc.scalar.copy(
+                out=dst[:, 8 * pair : 8 * pair + 8],
+                in_=src[:].rearrange("p u i (q t r) -> p (i q) t r u", t=PACK, r=RUN),
+            )
+
+        def turn_basis(j, kg):
+            for pair in range(2):
+                turn_pair(j, kg, pair)
+
+        def copy_basis(j, kg):
+            for pair in range(2):
+                copy_pair(j, kg, pair)
+
+        def quant_basis(j, kg, c0=0, cn=PASS):
             quantize(
                 b_codes[:, j, kg, c0 : c0 + cn],
                 b_plane[:, j, kg, c0 : c0 + cn],
                 b_bf[j][:, kg, PACK * c0 : PACK * (c0 + cn)],
             )
 
-        def sort_t(j):
-            nc.vector.tensor_copy(
-                out=t_codes[:, j].bitcast(I32).rearrange("p t g (q x) -> p t g q x", x=4),
-                in_=t_raw[:, j].bitcast(I32).rearrange("p g (q t x) -> p t g q x", t=PACK, x=4),
-            )
-
-        def sort_t_plane():
-            nc.vector.tensor_copy(
-                out=t_plane[:].bitcast(I32).rearrange("p t g j (q x) -> p t g (j q) x", x=2),
-                in_=t_plane_raw[:].bitcast(I32).rearrange("p g (b t x) -> p t g b x", t=PACK, x=2),
-            )
-
-        def stage_one(key, c, stationary):
-            bank = new_bank([P, PACK, CW])
-            cols = slice(CW * c, CW * (c + 1))
-            for t in range(PACK):
-                for kg in range(KG):
-                    codes, plane = stationary(t, kg)
-                    nc.tensor.matmul_mx(
-                        out=bank[:, t, :],
-                        lhsT=codes,
-                        lhsT_scale=plane,
-                        rhs=c_codes[:, kg, cols].bitcast(FP8X4),
-                        rhs_scale=c_plane[:, kg, cols],
-                        start=(kg == 0),
-                        stop=(kg == KG - 1),
-                    )
-            banks[key] = bank
-
-        def psi(j, c):
-            stage_one(
-                ("psi", j, c),
-                c,
-                lambda t, kg: (
-                    b_codes[:, j, kg, P * t : P * (t + 1)].bitcast(FP8X4),
-                    b_plane[:, j, kg, P * t : P * (t + 1)],
-                ),
-            )
-
-        def kin(j, c):
-            stage_one(
-                ("kin", j, c),
-                c,
-                lambda t, kg: (
-                    t_codes[:, j, t, kg, :].bitcast(FP4X4),
-                    t_plane[:, t, kg, j, :],
-                ),
-            )
-
-        def scale_v(j, c):
-            if (j, c // 4) not in vpsi:
-                vpsi[j, c // 4] = staged("vpsi", [P, PACK, PASS], F32, 5)
-            for t in range(PACK):
-                nc.scalar.activation(
-                    out=vpsi[j, c // 4][:, t, CW * (c % 4) : CW * (c % 4 + 1)],
-                    in_=banks["psi", j, c][:, t, :],
-                    func=COPY,
-                    scale=vw[:, j, t : t + 1],
+        def sort_t(j, j0, j1):
+            if j == 0:
+                nc.vector.tensor_copy(
+                    out=t_codes[:, :, j0:j1].bitcast(I32).rearrange("p t j g (q x) -> p t (j g q) x", x=4),
+                    in_=t_raw[:, j0:j1].bitcast(I32).rearrange("p j g (q t x) -> p t (j g q) x", t=PACK, x=4),
                 )
 
-        def left(j, c):
-            h, cc = divmod(c, 4)
-            if (j, h) not in l_bf:
-                l_bf[j, h] = staged("l_bf", [P, PACK, P, PACK], BF16, 3)
-            weight = vw[:, GG + j, :].rearrange("p (a b t) -> p a b t", a=1, b=1)
-            nc.vector.tensor_tensor(
-                out=l_bf[j, h][:, :, 32 * cc : 32 * (cc + 1), :],
-                in0=banks["psi", j, c][:].rearrange("p t (m s) -> p s m t", s=PACK),
-                in1=weight.to_broadcast([P, PACK, 32, PACK]),
-                op=MULT,
-            )
+        def sort_t_plane(j):
+            if j == 0:
+                nc.vector.tensor_copy(
+                    out=t_plane[:].bitcast(I32).rearrange("p t g j (q x) -> p t g (j q) x", x=2),
+                    in_=t_plane_raw[:].bitcast(I32).rearrange("p g (b t x) -> p t g b x", t=PACK, x=2),
+                )
 
-        def wide_step(j, h, t):
-            bank = new_bank([P, PASS])
-            cols = slice(PASS * h, PASS * (h + 1))
+        def times_c(out, codes, plane, cols):
             for kg in range(KG):
                 nc.tensor.matmul_mx(
-                    out=bank[:],
-                    lhsT=b_codes[:, j, kg, P * t : P * (t + 1)].bitcast(FP8X4),
-                    lhsT_scale=b_plane[:, j, kg, P * t : P * (t + 1)],
+                    out=out,
+                    lhsT=codes(kg),
+                    lhsT_scale=plane(kg),
                     rhs=c_codes[:, kg, cols].bitcast(FP8X4),
                     rhs_scale=c_plane[:, kg, cols],
                     start=(kg == 0),
                     stop=(kg == KG - 1),
                 )
-            banks["wide", j, h, t] = bank
 
-        def wide_act(j, h, t):
-            bank = banks.pop(("wide", j, h, t))
-            if (j, h) not in vpsi:
-                vpsi[j, h] = staged("vpsi", [P, PACK, PASS], F32, 5)
-                l_rows[j, h] = staged("big", [P, PACK, PASS], BF16, 5)
+        def psi_slot(out, j, t, cols):
+            points = slice(P * t, P * (t + 1))
+            times_c(
+                out, lambda kg: b_codes[:, j, kg, points].bitcast(FP8X4), lambda kg: b_plane[:, j, kg, points], cols
+            )
+
+        def psi_narrow(j, c):
+            bank = new_bank([P, PACK, CW])
+            for t in range(PACK):
+                psi_slot(bank[:, t, :], j, t, slice(CW * c, CW * (c + 1)))
+            banks["narrow", j, c] = bank
+
+        def left_narrow(j, c):
+            if c == 0:
+                l_bf[j, 0] = staged("woven", [P, PACK, P, PACK], BF16)
+            per = CW // PACK
+            weight = vw[:, GG + j, :].rearrange("p (a b t) -> p a b t", a=1, b=1)
+            nc.vector.tensor_tensor(
+                out=l_bf[j, 0][:, :, per * c : per * (c + 1), :],
+                in0=banks["narrow", j, c][:].rearrange("p t (m s) -> p s m t", s=PACK),
+                in1=weight.to_broadcast([P, PACK, per, PACK]),
+                op=MULT,
+            )
+
+        def vpsi_narrow(j, c):
+            if c == 0:
+                vpsi[j, 0] = staged("vpsi", [P, PACK, PASS], F32)
+            bank = banks.pop(("narrow", j, c))
+            for t in range(PACK):
+                nc.scalar.activation(
+                    out=vpsi[j, 0][:, t, CW * c : CW * (c + 1)],
+                    in_=bank[:, t, :],
+                    func=COPY,
+                    scale=vw[:, j, t : t + 1],
+                )
+
+        def psi_wide(j, t):
+            bank = new_bank([P, PASS])
+            psi_slot(bank[:], j, t, slice(PASS, 2 * PASS))
+            banks["wide", j, t] = bank
+
+        def scale_wide(j, t):
+            if t == 0:
+                vpsi[j, 1] = staged("vpsi", [P, PACK, PASS], F32)
+                l_rows[j] = staged("big", [P, PACK, PASS], BF16)
+            bank = banks.pop(("wide", j, t))
             nc.scalar.activation(
-                out=l_rows[j, h][:, t, :].rearrange("p (s m) -> p s m", s=PACK),
+                out=l_rows[j][:, t, :].rearrange("p (s m) -> p s m", s=PACK),
                 in_=bank[:].rearrange("p (m s) -> p s m", s=PACK),
                 func=COPY,
                 scale=vw[:, GG + j, t : t + 1],
             )
-            nc.scalar.activation(out=vpsi[j, h][:, t, :], in_=bank[:], func=COPY, scale=vw[:, j, t : t + 1])
+            nc.scalar.activation(out=vpsi[j, 1][:, t, :], in_=bank[:], func=COPY, scale=vw[:, j, t : t + 1])
 
-        def weave_left(j, h):
-            l_bf[j, h] = staged("l_bf", [P, PACK, P, PACK], BF16, 3)
+        def weave_left(j):
+            l_bf[j, 1] = staged("woven", [P, PACK, P, PACK], BF16)
             nc.vector.tensor_copy(
-                out=l_bf[j, h][:].rearrange("p s (c i) t -> p (s c) t i", i=4),
-                in_=l_rows.pop((j, h))[:].rearrange("p t (c i) -> p c t i", i=4),
+                out=l_bf[j, 1][:].rearrange("p s (c i) t -> p (s c) t i", i=4),
+                in_=l_rows.pop(j)[:].rearrange("p t (c i) -> p c t i", i=4),
             )
 
         def quant_left(j, h):
             cols = slice(PASS * h, PASS * (h + 1))
             quantize(l_codes[:, j, cols], l_plane[:, j, cols], l_bf.pop((j, h))[:].rearrange("p s m t -> p (s m t)"))
 
-        def slab_of(c):
-            return [s for s, (c0, cn) in enumerate(HQ) if c0 <= CW * c < c0 + cn][0]
+        def kin(j, c):
+            bank = new_bank([P, PACK, CW])
+            for t in range(PACK):
+                times_c(
+                    bank[:, t, :],
+                    lambda kg: t_codes[:, t, j, kg, :].bitcast(FP4X4),
+                    lambda kg: t_plane[:, t, kg, j, :],
+                    slice(CW * c, CW * (c + 1)),
+                )
+            banks["kin", j, c] = bank
 
         def hpsi(j, c):
-            s = slab_of(c)
-            c0, cn = HQ[s]
+            s = [n for n, (c0, cn) in enumerate(SLABS) if c0 <= CW * c < c0 + cn][0]
+            c0, cn = SLABS[s]
             if (j, s) not in h_bf:
-                h_bf[j, s] = staged("h_bf", [P, cn, PACK], BF16, 4)
+                h_bf[j, s] = staged("h_bf", [P, cn, PACK], BF16)
+            h, i = divmod(c, PACK)
             off = CW * c - c0
             nc.vector.tensor_tensor(
                 out=h_bf[j, s][:, off : off + CW, :].rearrange("p (c i) t -> p c t i", i=2),
                 in0=banks.pop(("kin", j, c))[:].rearrange("p t (c i) -> p c t i", i=2),
-                in1=vpsi[j, c // 4][:, :, CW * (c % 4) : CW * (c % 4 + 1)].rearrange("p t (c i) -> p c t i", i=2),
+                in1=vpsi[j, h][:, :, CW * i : CW * (i + 1)].rearrange("p t (c i) -> p c t i", i=2),
                 op=ADD,
             )
 
         def quant_hpsi(j, s):
-            c0, cn = HQ[s]
+            c0, cn = SLABS[s]
             cols = slice(c0, c0 + cn)
             quantize(h_codes[:, j, cols], h_plane[:, j, cols], h_bf.pop((j, s))[:].rearrange("p c t -> p (c t)"))
 
-        def scale_a(s, h):
-            c0, cn = PASS * s, PASS
-            da[s, h] = staged("big", [P, PACK, cn], F32, 5)
-            for t in range(PACK):
+        def scale_a(h, pair):
+            da[h, pair] = staged("big", [P, 2, N], F32)
+            for i in range(2):
+                t = 2 * pair + i
                 nc.scalar.activation(
-                    out=da[s, h][:, t, :],
-                    in_=rows_in["a", h][:, t, c0 : c0 + cn],
-                    func=COPY,
-                    scale=d_col[:, h, t : t + 1],
+                    out=da[h, pair][:, i, :], in_=a_rows[h][:, t, :], func=COPY, scale=d_col[:, h, t : t + 1]
                 )
 
         def slots(s, b):
-            per_bank = [1, 2, 4, 2, 2][s]
+            per_bank = PASS // SLABS[s][1]
             return range(per_bank * b, per_bank * (b + 1))
 
         def rayleigh(s, h, b):
             c0, cn = SLABS[s]
             cols = slice(c0, c0 + cn)
-            bank = new_bank([P, len(slots(s, b)), cn])
+            bank = new_bank([P, PASS // cn, cn])
             for i, t in enumerate(slots(s, b)):
-                rows = slice(PASS * h + P * t, PASS * h + P * (t + 1))
+                bands = slice(PASS * h + P * t, PASS * h + P * (t + 1))
                 for j in range(GG):
                     nc.tensor.matmul_mx(
                         out=bank[:, i, :],
-                        lhsT=l_codes[:, j, rows].bitcast(FP8X4),
-                        lhsT_scale=l_plane[:, j, rows],
+                        lhsT=l_codes[:, j, bands].bitcast(FP8X4),
+                        lhsT_scale=l_plane[:, j, bands],
                         rhs=h_codes[:, j, cols].bitcast(FP8X4),
                         rhs_scale=h_plane[:, j, cols],
                         start=(j == 0),
@@ -306,54 +296,52 @@ def tile_weighted_rayleigh_matrix_k4_kernel(
 
         def finish_y(s, h, b):
             c0, cn = SLABS[s]
-            if (s, h) not in y_f32:
-                y_f32[s, h] = staged(["rows", "big"][h] if cn == PASS else "y_f32", [P, PACK, cn], F32, [3, 5][h] if cn == PASS else 5)
+            if b == 0:
+                y_f32[s, h] = staged(["rows", "big"][h] if cn == PASS else "y_f32", [P, PACK, cn], F32)
             bank = banks.pop(("r", s, h, b))
             for i, t in enumerate(slots(s, b)):
                 nc.vector.scalar_tensor_tensor(
                     out=y_f32[s, h][:, t, :],
                     in0=bank[:, i, :],
                     scalar=d_col[:, h, t : t + 1],
-                    in1=da[c0 // PASS, h][:, t, c0 % PASS : c0 % PASS + cn],
+                    in1=da[h, t // 2][:, t % 2, c0 : c0 + cn],
                     op0=MULT,
                     op1=ADD,
                 )
 
-        def store_y(s, h):
-            c0, cn = SLABS[s]
-            dst = out_0[PASS * h : PASS * (h + 1), c0 : c0 + cn]
-            nc.sync.dma_start(out=dst.rearrange("(p t) m -> p t m", t=PACK), in_=y_f32[s, h][:])
-
-        def store_row(s, h, t):
+        def store_y(s, h, t0, t1):
             c0, cn = SLABS[s]
             dst = out_0[PASS * h : PASS * (h + 1), c0 : c0 + cn].rearrange("(p t) m -> p t m", t=PACK)
-            nc.sync.dma_start(out=dst[:, t, :], in_=y_f32[s, h][:, t, :])
+            nc.sync.dma_start(out=dst[:, t0:t1, :], in_=y_f32[s, h][:, t0:t1, :])
 
-        def round_y(s, h, on_vector):
-            c0, cn = SLABS[s]
-            y_bf[s, h] = staged("l_bf", [P, cn, PACK], BF16, 3)
+        def round_y(s, h, shared):
+            cn = SLABS[s][1]
+            y_bf[s, h] = staged("woven", [P, cn, PACK], BF16)
             dst = y_bf[s, h][:].rearrange("p (c i) t -> p c t i", i=2)
             src = y_f32[s, h][:].rearrange("p t (c i) -> p c t i", i=2)
-            if on_vector:
-                nc.vector.tensor_copy(out=dst, in_=src)
+            if shared:
+                cut = cn // 4
+                nc.scalar.copy(out=dst[:, :cut], in_=src[:, :cut])
+                nc.vector.tensor_copy(out=dst[:, cut:], in_=src[:, cut:])
             else:
                 nc.scalar.copy(out=dst, in_=src)
+
+        def store_scales(c0, cn, queues):
+            for quad in range(4):
+                queues[quad % len(queues)].dma_start(
+                    out=out_2[:, 4 * quad : 4 * quad + 4, c0 : c0 + cn].rearrange("g r n -> r g n").bitcast(I32),
+                    in_=y_plane[32 * quad : 32 * quad + 4, :, c0 : c0 + cn].bitcast(I32),
+                )
 
         def quant_y(s, h):
             c0, cn = SLABS[s]
             cols = slice(c0, c0 + cn)
             quantize(y_codes[:, h, cols], y_plane[:, h, cols], y_bf.pop((s, h))[:].rearrange("p c t -> p (c t)"))
-
-        def store_codes(c0, cn):
-            dst = out_1.rearrange("h p m t -> p h (m t)")[:, :, PACK * c0 : PACK * (c0 + cn)]
-            nc.sync.dma_start(out=dst.bitcast(I32), in_=y_codes[:, :, c0 : c0 + cn].bitcast(I32))
-
-        def store_scales(c0, cn, queues):
-            for q in range(4):
-                queues[q % len(queues)].dma_start(
-                    out=out_2[:, 4 * q : 4 * q + 4, c0 : c0 + cn].rearrange("g r n -> r g n").bitcast(I32),
-                    in_=y_plane[32 * q : 32 * q + 4, :, c0 : c0 + cn].bitcast(I32),
-                )
+            if h == NG - 1:
+                dst = out_1.rearrange("h p m t -> p h (m t)")[:, :, PACK * c0 : PACK * (c0 + cn)]
+                nc.sync.dma_start(out=dst.bitcast(I32), in_=y_codes[:, :, cols].bitcast(I32))
+                if s == 0:
+                    store_scales(c0, cn, [nc.sync])
 
         nc.vector.memset(vw_rows[:], 0.0)
         nc.vector.memset(c_plane[:].bitcast(I32), 0)
@@ -362,269 +350,96 @@ def tile_weighted_rayleigh_matrix_k4_kernel(
         nc.gpsimd.dma_start(out=vw_rows[0:GG, :], in_=v.rearrange("(j g) -> j g", j=GG))
         nc.gpsimd.dma_start(out=vw_rows[GG : 2 * GG, :], in_=w.rearrange("(j g) -> j g", j=GG))
         for kg in range(KG):
-            for ip in range(2):
-                load_basis(0, kg, 2 * ip, 2)
-        load_plane(nc.sync, c_plane, c_scales)
+            for pair in range(2):
+                load_basis(0, kg, 2 * pair, 2)
+        load_plane(c_plane, c_scales)
         load_c(0)
-        load_basis(1, 0, 0, 4)
+        load_basis(1, 0, 0, PACK)
         load_c(2)
         load_c(3)
-        load_plane(nc.sync, t_plane_raw, t_scales)
+        load_plane(t_plane_raw, t_scales)
         load_t(0)
         load_c(1)
-        load_basis(1, 1, 0, 4)
+        load_basis(1, 1, 0, PACK)
         load_t(1)
         load_t(2)
-        load_basis(2, 0, 0, 4)
-        load_basis(2, 1, 0, 4)
+        for kg in range(KG):
+            load_basis(2, kg, 0, PACK)
         nc.sync.dma_start(out=d_raw[:], in_=d.rearrange("(h p t) -> p h t", p=P, t=PACK))
-        load_a(0)
-        load_a(1)
+        for h in range(NG):
+            load_a(h)
 
-        for ip in range(2):
-            turn_basis(0, 0, ip)
-            copy_basis(0, 0, ip)
-        quant_basis(0, 0, 0, PASS)
+        for pair in range(2):
+            turn_pair(0, 0, pair)
+            copy_pair(0, 0, pair)
+        quant_basis(0, 0)
         nc.vector.tensor_copy(
-            out=vw_sorted[:].rearrange("p t (q r) -> p t q r", r=8),
-            in_=vw_rows[:].rearrange("p (q t r) -> p t q r", t=PACK, r=8),
+            out=vw_sorted[:].rearrange("p t (q r) -> p t q r", r=RUN),
+            in_=vw_rows[:].rearrange("p (q t r) -> p t q r", t=PACK, r=RUN),
         )
-        for ip in range(2):
-            turn_basis(0, 1, ip)
-            copy_basis(0, 1, ip)
+        for pair in range(2):
+            turn_pair(0, 1, pair)
+            copy_pair(0, 1, pair)
         vw_bank = new_bank([P, PACK, P])
         for t in range(PACK):
             nc.tensor.transpose(vw_bank[:, t, :], vw_sorted[:, t, :], ident[:])
-        quant_basis(0, 1, 0, 256)
-        quant_basis(0, 1, 256, 256)
+        for c0 in (0, PASS // 2):
+            quant_basis(0, 1, c0, PASS // 2)
         nc.vector.tensor_copy(out=vw[:], in_=vw_bank[:, :, 0 : 2 * GG].rearrange("p t c -> p c t"))
 
-        def widen_d(j):
-            nc.scalar.activation(out=d_col[:], in_=d_raw[:], func=COPY)
+        round_steps = [
+            (0, psi_narrow, 0), (1, turn_basis, 0), (0, sort_t_plane), (0, sort_t, 0, 1), (0, left_narrow, 0),
+            (1, copy_basis, 0), (0, psi_wide, 0), (0, psi_narrow, 1), (0, scale_wide, 0), (-1, kin, 4),
+            (-1, hpsi, 4), (0, psi_narrow, 2), (0, vpsi_narrow, 0), (0, left_narrow, 1), (0, psi_narrow, 3),
+            (0, vpsi_narrow, 1), (0, left_narrow, 2), (-1, kin, 5), (0, vpsi_narrow, 2), (0, left_narrow, 3),
+            (0, kin, 0), (-1, hpsi, 5), (0, psi_wide, 1), (0, hpsi, 0), (0, scale_wide, 1), (0, kin, 1),
+            (0, quant_left, 0), (1, turn_basis, 1), (0, hpsi, 1), (0, sort_t, 1, GG), (1, copy_basis, 1),
+            (-1, quant_left, 1), (0, psi_wide, 2), (1, quant_basis, 0), (0, vpsi_narrow, 3), (0, kin, 2),
+            (0, scale_wide, 2), (0, kin, 3), (1, quant_basis, 1), (0, hpsi, 2), (0, psi_wide, 3), (0, hpsi, 3),
+            (-1, quant_hpsi, 1), (0, scale_wide, 3), (0, quant_hpsi, 0), (0, weave_left),
+        ]
+        for r in range(GG + 1):
+            for entry in round_steps:
+                lag, step, args = entry[0], entry[1], entry[2:]
+                if 0 <= r + lag < GG:
+                    step(r + lag, *args)
 
-        def sort_plane(j):
-            sort_t_plane()
+        nc.scalar.activation(out=d_col[:], in_=d_raw[:], func=COPY)
+        for h in range(NG):
+            for pair in range(2):
+                scale_a(h, pair)
 
-        def turn_half(j, kg):
-            for ip in range(2):
-                turn_basis(j, kg, ip)
+        tiles = [(s, h) for s in range(len(SLABS)) for h in range(NG)]
+        r_banks = [(s, h, b) for s, h in tiles for b in range(PACK * SLABS[s][1] // PASS)]
+        last_slab = len(SLABS) - 1
+        last_chunks = range(SLABS[last_slab][0] // CW, N // CW)
+        late = [(j, c) for j in range(GG) for c in last_chunks]
 
-        def copy_half(j, kg):
-            for ip in range(2):
-                copy_basis(j, kg, ip)
+        def finish_bank(s, h, b):
+            finish_y(s, h, b)
+            complete = slots(s, b).stop == PACK
+            if s == 0:
+                store_y(s, h, b, b + 1)
+            elif complete:
+                store_y(s, h, 0, PACK)
+            if complete:
+                round_y(s, h, (s, h) == tiles[-1])
+            n = tiles.index((s, h))
+            if b == 0 and n >= 2:
+                quant_y(*tiles[n - 2])
 
-        def kin_step(j, c):
-            kin(j, c)
-            hpsi(j, c)
-
-        psi(0, 0)
-        turn_half(1, 0)
-        sort_plane(0)
-        sort_t(0)
-        left(0, 0)
-        copy_half(1, 0)
-        wide_step(0, 1, 0)
-        psi(0, 1)
-        wide_act(0, 1, 0)
-        psi(0, 2)
-        scale_v(0, 0)
-        left(0, 1)
-        psi(0, 3)
-        scale_v(0, 1)
-        left(0, 2)
-        scale_v(0, 2)
-        left(0, 3)
-        kin(0, 0)
-        wide_step(0, 1, 1)
-        hpsi(0, 0)
-        wide_act(0, 1, 1)
-        kin(0, 1)
-        quant_left(0, 0)
-        turn_half(1, 1)
-        hpsi(0, 1)
-        copy_half(1, 1)
-        wide_step(0, 1, 2)
-        quant_basis(1, 0, 0, PASS)
-        scale_v(0, 3)
-        kin(0, 2)
-        quant_hpsi(0, 0)
-        wide_act(0, 1, 2)
-        kin(0, 3)
-        quant_basis(1, 1, 0, PASS)
-        hpsi(0, 2)
-        wide_step(0, 1, 3)
-        hpsi(0, 3)
-        wide_act(0, 1, 3)
-        quant_hpsi(0, 1)
-        weave_left(0, 1)
-        psi(1, 0)
-        turn_half(2, 0)
-        sort_t(1)
-        left(1, 0)
-        copy_half(2, 0)
-        wide_step(1, 1, 0)
-        psi(1, 1)
-        wide_act(1, 1, 0)
-        kin(0, 4)
-        hpsi(0, 4)
-        psi(1, 2)
-        scale_v(1, 0)
-        left(1, 1)
-        psi(1, 3)
-        scale_v(1, 1)
-        left(1, 2)
-        kin(0, 5)
-        scale_v(1, 2)
-        left(1, 3)
-        kin(1, 0)
-        hpsi(0, 5)
-        wide_step(1, 1, 1)
-        hpsi(1, 0)
-        wide_act(1, 1, 1)
-        kin(1, 1)
-        quant_left(1, 0)
-        turn_half(2, 1)
-        hpsi(1, 1)
-        copy_half(2, 1)
-        quant_left(0, 1)
-        wide_step(1, 1, 2)
-        quant_basis(2, 0, 0, PASS)
-        scale_v(1, 3)
-        kin(1, 2)
-        quant_hpsi(1, 0)
-        wide_act(1, 1, 2)
-        kin(1, 3)
-        quant_basis(2, 1, 0, PASS)
-        hpsi(1, 2)
-        wide_step(1, 1, 3)
-        hpsi(1, 3)
-        quant_hpsi(0, 2)
-        wide_act(1, 1, 3)
-        quant_hpsi(1, 1)
-        weave_left(1, 1)
-        psi(2, 0)
-        sort_t(2)
-        left(2, 0)
-        wide_step(2, 1, 0)
-        psi(2, 1)
-        wide_act(2, 1, 0)
-        kin(1, 4)
-        hpsi(1, 4)
-        psi(2, 2)
-        scale_v(2, 0)
-        left(2, 1)
-        psi(2, 3)
-        scale_v(2, 1)
-        left(2, 2)
-        kin(1, 5)
-        scale_v(2, 2)
-        left(2, 3)
-        kin(2, 0)
-        hpsi(1, 5)
-        wide_step(2, 1, 1)
-        hpsi(2, 0)
-        wide_act(2, 1, 1)
-        kin(2, 1)
-        quant_left(2, 0)
-        hpsi(2, 1)
-        quant_left(1, 1)
-        wide_step(2, 1, 2)
-        scale_v(2, 3)
-        kin(2, 2)
-        quant_hpsi(2, 0)
-        wide_act(2, 1, 2)
-        kin(2, 3)
-        hpsi(2, 2)
-        wide_step(2, 1, 3)
-        hpsi(2, 3)
-        quant_hpsi(1, 2)
-        wide_act(2, 1, 3)
-        quant_hpsi(2, 1)
-        weave_left(2, 1)
-        kin(2, 4)
-        hpsi(2, 4)
-        kin(2, 5)
-        hpsi(2, 5)
-        quant_left(2, 1)
-        quant_hpsi(2, 2)
-        widen_d(0)
-        scale_a(0, 0)
-        scale_a(0, 1)
-        scale_a(1, 0)
-        scale_a(1, 1)
-        kin(0, 6)
-        kin(0, 7)
-        hpsi(0, 6)
-        rayleigh(0, 0, 0)
-        hpsi(0, 7)
-        kin(1, 6)
-        finish_y(0, 0, 0)
-        store_row(0, 0, 0)
-        rayleigh(0, 0, 1)
-        hpsi(1, 6)
-        quant_hpsi(0, 3)
-        kin(1, 7)
-        finish_y(0, 0, 1)
-        store_row(0, 0, 1)
-        rayleigh(0, 0, 2)
-        hpsi(1, 7)
-        rayleigh(0, 0, 3)
-        finish_y(0, 0, 2)
-        store_row(0, 0, 2)
-        quant_hpsi(1, 3)
-        kin(2, 6)
-        finish_y(0, 0, 3)
-        store_row(0, 0, 3)
-        round_y(0, 0, False)
-        rayleigh(0, 1, 0)
-        hpsi(2, 6)
-        kin(2, 7)
-        finish_y(0, 1, 0)
-        store_row(0, 1, 0)
-        rayleigh(0, 1, 1)
-        hpsi(2, 7)
-        rayleigh(0, 1, 2)
-        finish_y(0, 1, 1)
-        store_row(0, 1, 1)
-        quant_hpsi(2, 3)
-        rayleigh(0, 1, 3)
-        finish_y(0, 1, 2)
-        store_row(0, 1, 2)
-        rayleigh(1, 0, 0)
-        finish_y(0, 1, 3)
-        store_row(0, 1, 3)
-        round_y(0, 1, False)
-        quant_y(0, 0)
-        rayleigh(1, 0, 1)
-        finish_y(1, 0, 0)
-        rayleigh(1, 1, 0)
-        finish_y(1, 0, 1)
-        store_y(1, 0)
-        round_y(1, 0, False)
-        rayleigh(1, 1, 1)
-        finish_y(1, 1, 0)
-        quant_y(0, 1)
-        store_codes(0, 512)
-        store_scales(0, 512, [nc.sync])
-        rayleigh(4, 0, 0)
-        finish_y(1, 1, 1)
-        store_y(1, 1)
-        round_y(1, 1, False)
-        quant_y(1, 0)
-        rayleigh(4, 0, 1)
-        finish_y(4, 0, 0)
-        rayleigh(4, 1, 0)
-        finish_y(4, 0, 1)
-        store_y(4, 0)
-        round_y(4, 0, False)
-        quant_y(1, 1)
-        store_codes(512, 256)
-        rayleigh(4, 1, 1)
-        finish_y(4, 1, 0)
-        finish_y(4, 1, 1)
-        round_y(4, 1, True)
-        store_y(4, 1)
-        quant_y(4, 0)
-        quant_y(4, 1)
-        store_codes(768, 256)
-        store_scales(512, 512, [nc.scalar, nc.sync])
+        kin(*late[0])
+        for n, r_bank in enumerate(r_banks):
+            if n + 1 < len(late):
+                kin(*late[n + 1])
+            rayleigh(*r_bank)
+            if n < len(late):
+                hpsi(*late[n])
+            if n > 0:
+                finish_bank(*r_banks[n - 1])
+            if n < len(late) and late[n][1] == last_chunks[-1]:
+                quant_hpsi(late[n][0], last_slab)
+        finish_bank(*r_banks[-1])
+        for tile in tiles[-2:]:
+            quant_y(*tile)
+        store_scales(SLABS[0][1], N - SLABS[0][1], [nc.scalar, nc.sync])

from contextlib import ExitStack

import concourse.mybir as mybir
from concourse.masks import make_identity

G, K, N = 1536, 1024, 1024
FLOPS = 2 * G * K * N * 2 + 2 * G * N * N

F32 = mybir.dt.float32
BF16 = mybir.dt.bfloat16
U32 = mybir.dt.uint32
I32 = mybir.dt.int32
U8 = mybir.dt.uint8
FP8X4 = mybir.dt.float8_e4m3fn_x4
FP4X4 = mybir.dt.float4_e2m1fn_x4
COPY = mybir.ActivationFunctionType.Copy
ADD = mybir.AluOpType.add
MULT = mybir.AluOpType.mult

P = 128
PACK = 4
PASS = P * PACK
RUN = 8
KG = K // PASS
GG = G // PASS
NG = N // PASS
CW = PASS // PACK
C_PIECE = 256
SLABS = [(0, 512), (512, 256), (768, 256)]


def tile_weighted_rayleigh_matrix_k4_kernel(
    tc, c_words, c_scales, t_words, t_scales, basis, v, w, a, d, out_0, out_1, out_2
):
    nc = tc.nc

    with ExitStack() as ctx:
        keep = ctx.enter_context(tc.tile_pool(name="keep", bufs=1))
        stage = ctx.enter_context(tc.tile_pool(name="stage", bufs=3))
        psum = ctx.enter_context(tc.psum_pool(name="psum", bufs=8))
        ctx.enter_context(tc.manual_schedule())

        def kept(name, shape, dtype):
            return keep.tile(shape, dtype, name=name, align_bytes=64)

        depth = {"rows": 3, "big": 5, "vpsi": 5, "woven": 3, "h_bf": 3, "y_f32": 4}

        def staged(tag, shape, dtype):
            return stage.tile(shape, dtype, name=tag, tag=tag, bufs=depth[tag], align_bytes=64)

        def new_bank(shape):
            return psum.tile(shape, F32, name="bank", tag="bank")

        ident = kept("ident", [P, P], F32)
        c_codes = kept("c_codes", [P, KG, N], U32)
        c_plane = kept("c_plane", [P, KG, N], U8)
        t_raw = kept("t_raw", [P, GG, KG, 2 * PASS], U8)
        t_codes = kept("t_codes", [P, PACK, GG, KG, 2 * P], U8)
        t_plane_raw = kept("t_plane_raw", [P, KG, G], U8)
        t_plane = kept("t_plane", [P, PACK, KG, GG, P], U8)
        b_codes = kept("b_codes", [P, GG, KG, PASS], U32)
        b_plane = kept("b_plane", [P, GG, KG, PASS], U8)
        l_codes = kept("l_codes", [P, GG, N], U32)
        l_plane = kept("l_plane", [P, GG, N], U8)
        h_codes = kept("h_codes", [P, GG, N], U32)
        h_plane = kept("h_plane", [P, GG, N], U8)
        y_codes = kept("y_codes", [P, NG, N], U32)
        y_plane = kept("y_plane", [P, NG, N], U8)
        vw_rows = kept("vw_rows", [P, PASS], BF16)
        vw_sorted = kept("vw_sorted", [P, PACK, P], F32)
        vw = kept("vw", [P, 2 * GG, PACK], F32)
        d_raw = kept("d_raw", [P, NG, PACK], BF16)
        d_col = kept("d_col", [P, NG, PACK], F32)

        b_rows, a_rows, b_bf, l_rows, l_bf, vpsi = {}, {}, {}, {}, {}, {}
        h_bf, da, y_f32, y_bf, banks = {}, {}, {}, {}, {}

        def load_basis(j, kg, i0, ni):
            if j not in b_rows:
                b_rows[j] = staged("rows", [P, PACK, K], BF16)
            src = basis[PASS * j + P * i0 : PASS * j + P * (i0 + ni), PASS * kg : PASS * (kg + 1)]
            nc.sync.dma_start(
                out=b_rows[j][:, i0 : i0 + ni, PASS * kg : PASS * (kg + 1)],
                in_=src.rearrange("(i p) k -> p i k", p=P),
            )

        def load_c(n):
            cols = slice(C_PIECE * n, C_PIECE * (n + 1))
            src = c_words.rearrange("g p n t -> p g (n t)")[:, :, PACK * cols.start : PACK * cols.stop]
            nc.sync.dma_start(out=c_codes[:, :, cols].bitcast(I32), in_=src.bitcast(I32))

        def load_t(j):
            src = t_words.rearrange("g p b -> p g b")[:, :, 2 * PASS * j : 2 * PASS * (j + 1)]
            nc.sync.dma_start(out=t_raw[:, j].bitcast(I32), in_=src.bitcast(I32))

        def load_a(h):
            a_rows[h] = staged("rows", [P, PACK, N], BF16)
            nc.sync.dma_start(
                out=a_rows[h][:], in_=a[PASS * h : PASS * (h + 1), :].rearrange("(p t) m -> p t m", t=PACK)
            )

        def load_plane(plane, scales):
            for quad in range(4):
                nc.sync.dma_start(
                    out=plane[32 * quad : 32 * quad + 4, :, :].bitcast(I32),
                    in_=scales[:, 4 * quad : 4 * quad + 4, :].rearrange("g r n -> r g n").bitcast(I32),
                )

        def quantize(codes, plane, values):
            nc.vector.quantize_mx(out=codes.bitcast(FP8X4), scales=plane, in_=values)

        def turn_pair(j, kg, pair):
            bank = new_bank([P, 2, 2, P])
            for i in range(2):
                words = b_rows[j][:, 2 * pair + i, :].bitcast(F32)
                first = kg * PASS // 2
                for u in range(2):
                    nc.tensor.transpose(bank[:, u, i, :], words[:, first + u : first + PASS // 2 : 2], ident[:])
            banks["basis", j, kg, pair] = bank

        def copy_pair(j, kg, pair):
            if j not in b_bf:
                b_bf[j] = staged("big", [P, KG, PASS * PACK], BF16)
            dst = b_bf[j][:, kg, :].bitcast(F32).rearrange("p (t q r u) -> p q t r u", t=PACK, r=RUN, u=2)
            src = banks.pop(("basis", j, kg, pair))
            nc.scalar.copy(
                out=dst[:, 8 * pair : 8 * pair + 8],
                in_=src[:].rearrange("p u i (q t r) -> p (i q) t r u", t=PACK, r=RUN),
            )

        def turn_basis(j, kg):
            for pair in range(2):
                turn_pair(j, kg, pair)

        def copy_basis(j, kg):
            for pair in range(2):
                copy_pair(j, kg, pair)

        def quant_basis(j, kg, c0=0, cn=PASS):
            quantize(
                b_codes[:, j, kg, c0 : c0 + cn],
                b_plane[:, j, kg, c0 : c0 + cn],
                b_bf[j][:, kg, PACK * c0 : PACK * (c0 + cn)],
            )

        def sort_t(j, j0, j1):
            if j == 0:
                nc.vector.tensor_copy(
                    out=t_codes[:, :, j0:j1].bitcast(I32).rearrange("p t j g (q x) -> p t (j g q) x", x=4),
                    in_=t_raw[:, j0:j1].bitcast(I32).rearrange("p j g (q t x) -> p t (j g q) x", t=PACK, x=4),
                )

        def sort_t_plane(j):
            if j == 0:
                nc.vector.tensor_copy(
                    out=t_plane[:].bitcast(I32).rearrange("p t g j (q x) -> p t g (j q) x", x=2),
                    in_=t_plane_raw[:].bitcast(I32).rearrange("p g (b t x) -> p t g b x", t=PACK, x=2),
                )

        def times_c(out, codes, plane, cols):
            for kg in range(KG):
                nc.tensor.matmul_mx(
                    out=out,
                    lhsT=codes(kg),
                    lhsT_scale=plane(kg),
                    rhs=c_codes[:, kg, cols].bitcast(FP8X4),
                    rhs_scale=c_plane[:, kg, cols],
                    start=(kg == 0),
                    stop=(kg == KG - 1),
                )

        def psi_slot(out, j, t, cols):
            points = slice(P * t, P * (t + 1))
            times_c(
                out, lambda kg: b_codes[:, j, kg, points].bitcast(FP8X4), lambda kg: b_plane[:, j, kg, points], cols
            )

        def psi_narrow(j, c):
            bank = new_bank([P, PACK, CW])
            for t in range(PACK):
                psi_slot(bank[:, t, :], j, t, slice(CW * c, CW * (c + 1)))
            banks["narrow", j, c] = bank

        def left_narrow(j, c):
            if c == 0:
                l_bf[j, 0] = staged("woven", [P, PACK, P, PACK], BF16)
            per = CW // PACK
            weight = vw[:, GG + j, :].rearrange("p (a b t) -> p a b t", a=1, b=1)
            nc.vector.tensor_tensor(
                out=l_bf[j, 0][:, :, per * c : per * (c + 1), :],
                in0=banks["narrow", j, c][:].rearrange("p t (m s) -> p s m t", s=PACK),
                in1=weight.to_broadcast([P, PACK, per, PACK]),
                op=MULT,
            )

        def vpsi_narrow(j, c):
            if c == 0:
                vpsi[j, 0] = staged("vpsi", [P, PACK, PASS], F32)
            bank = banks.pop(("narrow", j, c))
            for t in range(PACK):
                nc.scalar.activation(
                    out=vpsi[j, 0][:, t, CW * c : CW * (c + 1)],
                    in_=bank[:, t, :],
                    func=COPY,
                    scale=vw[:, j, t : t + 1],
                )

        def psi_wide(j, t):
            bank = new_bank([P, PASS])
            psi_slot(bank[:], j, t, slice(PASS, 2 * PASS))
            banks["wide", j, t] = bank

        def scale_wide(j, t):
            if t == 0:
                vpsi[j, 1] = staged("vpsi", [P, PACK, PASS], F32)
                l_rows[j] = staged("big", [P, PACK, PASS], BF16)
            bank = banks.pop(("wide", j, t))
            nc.scalar.activation(
                out=l_rows[j][:, t, :].rearrange("p (s m) -> p s m", s=PACK),
                in_=bank[:].rearrange("p (m s) -> p s m", s=PACK),
                func=COPY,
                scale=vw[:, GG + j, t : t + 1],
            )
            nc.scalar.activation(out=vpsi[j, 1][:, t, :], in_=bank[:], func=COPY, scale=vw[:, j, t : t + 1])

        def weave_left(j):
            l_bf[j, 1] = staged("woven", [P, PACK, P, PACK], BF16)
            nc.vector.tensor_copy(
                out=l_bf[j, 1][:].rearrange("p s (c i) t -> p (s c) t i", i=4),
                in_=l_rows.pop(j)[:].rearrange("p t (c i) -> p c t i", i=4),
            )

        def quant_left(j, h):
            cols = slice(PASS * h, PASS * (h + 1))
            quantize(l_codes[:, j, cols], l_plane[:, j, cols], l_bf.pop((j, h))[:].rearrange("p s m t -> p (s m t)"))

        def kin(j, c):
            bank = new_bank([P, PACK, CW])
            for t in range(PACK):
                times_c(
                    bank[:, t, :],
                    lambda kg: t_codes[:, t, j, kg, :].bitcast(FP4X4),
                    lambda kg: t_plane[:, t, kg, j, :],
                    slice(CW * c, CW * (c + 1)),
                )
            banks["kin", j, c] = bank

        def hpsi(j, c):
            s = [n for n, (c0, cn) in enumerate(SLABS) if c0 <= CW * c < c0 + cn][0]
            c0, cn = SLABS[s]
            if (j, s) not in h_bf:
                h_bf[j, s] = staged("h_bf", [P, cn, PACK], BF16)
            h, i = divmod(c, PACK)
            off = CW * c - c0
            nc.vector.tensor_tensor(
                out=h_bf[j, s][:, off : off + CW, :].rearrange("p (c i) t -> p c t i", i=2),
                in0=banks.pop(("kin", j, c))[:].rearrange("p t (c i) -> p c t i", i=2),
                in1=vpsi[j, h][:, :, CW * i : CW * (i + 1)].rearrange("p t (c i) -> p c t i", i=2),
                op=ADD,
            )

        def quant_hpsi(j, s):
            c0, cn = SLABS[s]
            cols = slice(c0, c0 + cn)
            quantize(h_codes[:, j, cols], h_plane[:, j, cols], h_bf.pop((j, s))[:].rearrange("p c t -> p (c t)"))

        def scale_a(h, pair):
            da[h, pair] = staged("big", [P, 2, N], F32)
            for i in range(2):
                t = 2 * pair + i
                nc.scalar.activation(
                    out=da[h, pair][:, i, :], in_=a_rows[h][:, t, :], func=COPY, scale=d_col[:, h, t : t + 1]
                )

        def slots(s, b):
            per_bank = PASS // SLABS[s][1]
            return range(per_bank * b, per_bank * (b + 1))

        def rayleigh(s, h, b):
            c0, cn = SLABS[s]
            cols = slice(c0, c0 + cn)
            bank = new_bank([P, PASS // cn, cn])
            for i, t in enumerate(slots(s, b)):
                bands = slice(PASS * h + P * t, PASS * h + P * (t + 1))
                for j in range(GG):
                    nc.tensor.matmul_mx(
                        out=bank[:, i, :],
                        lhsT=l_codes[:, j, bands].bitcast(FP8X4),
                        lhsT_scale=l_plane[:, j, bands],
                        rhs=h_codes[:, j, cols].bitcast(FP8X4),
                        rhs_scale=h_plane[:, j, cols],
                        start=(j == 0),
                        stop=(j == GG - 1),
                    )
            banks["r", s, h, b] = bank

        def finish_y(s, h, b):
            c0, cn = SLABS[s]
            if b == 0:
                y_f32[s, h] = staged(["rows", "big"][h] if cn == PASS else "y_f32", [P, PACK, cn], F32)
            bank = banks.pop(("r", s, h, b))
            for i, t in enumerate(slots(s, b)):
                nc.vector.scalar_tensor_tensor(
                    out=y_f32[s, h][:, t, :],
                    in0=bank[:, i, :],
                    scalar=d_col[:, h, t : t + 1],
                    in1=da[h, t // 2][:, t % 2, c0 : c0 + cn],
                    op0=MULT,
                    op1=ADD,
                )

        def store_y(s, h, t0, t1):
            c0, cn = SLABS[s]
            dst = out_0[PASS * h : PASS * (h + 1), c0 : c0 + cn].rearrange("(p t) m -> p t m", t=PACK)
            nc.sync.dma_start(out=dst[:, t0:t1, :], in_=y_f32[s, h][:, t0:t1, :])

        def round_y(s, h, shared):
            cn = SLABS[s][1]
            y_bf[s, h] = staged("woven", [P, cn, PACK], BF16)
            dst = y_bf[s, h][:].rearrange("p (c i) t -> p c t i", i=2)
            src = y_f32[s, h][:].rearrange("p t (c i) -> p c t i", i=2)
            if shared:
                cut = cn // 4
                nc.scalar.copy(out=dst[:, :cut], in_=src[:, :cut])
                nc.vector.tensor_copy(out=dst[:, cut:], in_=src[:, cut:])
            else:
                nc.scalar.copy(out=dst, in_=src)

        def store_scales(c0, cn, queues):
            for quad in range(4):
                queues[quad % len(queues)].dma_start(
                    out=out_2[:, 4 * quad : 4 * quad + 4, c0 : c0 + cn].rearrange("g r n -> r g n").bitcast(I32),
                    in_=y_plane[32 * quad : 32 * quad + 4, :, c0 : c0 + cn].bitcast(I32),
                )

        def quant_y(s, h):
            c0, cn = SLABS[s]
            cols = slice(c0, c0 + cn)
            quantize(y_codes[:, h, cols], y_plane[:, h, cols], y_bf.pop((s, h))[:].rearrange("p c t -> p (c t)"))
            if h == NG - 1:
                dst = out_1.rearrange("h p m t -> p h (m t)")[:, :, PACK * c0 : PACK * (c0 + cn)]
                nc.sync.dma_start(out=dst.bitcast(I32), in_=y_codes[:, :, cols].bitcast(I32))
                if s == 0:
                    store_scales(c0, cn, [nc.sync])

        nc.vector.memset(vw_rows[:], 0.0)
        nc.vector.memset(c_plane[:].bitcast(I32), 0)
        nc.vector.memset(t_plane_raw[:].bitcast(I32), 0)
        make_identity(nc, ident[:])
        nc.gpsimd.dma_start(out=vw_rows[0:GG, :], in_=v.rearrange("(j g) -> j g", j=GG))
        nc.gpsimd.dma_start(out=vw_rows[GG : 2 * GG, :], in_=w.rearrange("(j g) -> j g", j=GG))
        for kg in range(KG):
            for pair in range(2):
                load_basis(0, kg, 2 * pair, 2)
        load_plane(c_plane, c_scales)
        load_c(0)
        load_basis(1, 0, 0, PACK)
        load_c(2)
        load_c(3)
        load_plane(t_plane_raw, t_scales)
        load_t(0)
        load_c(1)
        load_basis(1, 1, 0, PACK)
        load_t(1)
        load_t(2)
        for kg in range(KG):
            load_basis(2, kg, 0, PACK)
        nc.sync.dma_start(out=d_raw[:], in_=d.rearrange("(h p t) -> p h t", p=P, t=PACK))
        for h in range(NG):
            load_a(h)

        for pair in range(2):
            turn_pair(0, 0, pair)
            copy_pair(0, 0, pair)
        quant_basis(0, 0)
        nc.vector.tensor_copy(
            out=vw_sorted[:].rearrange("p t (q r) -> p t q r", r=RUN),
            in_=vw_rows[:].rearrange("p (q t r) -> p t q r", t=PACK, r=RUN),
        )
        for pair in range(2):
            turn_pair(0, 1, pair)
            copy_pair(0, 1, pair)
        vw_bank = new_bank([P, PACK, P])
        for t in range(PACK):
            nc.tensor.transpose(vw_bank[:, t, :], vw_sorted[:, t, :], ident[:])
        for c0 in (0, PASS // 2):
            quant_basis(0, 1, c0, PASS // 2)
        nc.vector.tensor_copy(out=vw[:], in_=vw_bank[:, :, 0 : 2 * GG].rearrange("p t c -> p c t"))

        round_steps = [
            (0, psi_narrow, 0), (1, turn_basis, 0), (0, sort_t_plane), (0, sort_t, 0, 1), (0, left_narrow, 0),
            (1, copy_basis, 0), (0, psi_wide, 0), (0, psi_narrow, 1), (0, scale_wide, 0), (-1, kin, 4),
            (-1, hpsi, 4), (0, psi_narrow, 2), (0, vpsi_narrow, 0), (0, left_narrow, 1), (0, psi_narrow, 3),
            (0, vpsi_narrow, 1), (0, left_narrow, 2), (-1, kin, 5), (0, vpsi_narrow, 2), (0, left_narrow, 3),
            (0, kin, 0), (-1, hpsi, 5), (0, psi_wide, 1), (0, hpsi, 0), (0, scale_wide, 1), (0, kin, 1),
            (0, quant_left, 0), (1, turn_basis, 1), (0, hpsi, 1), (0, sort_t, 1, GG), (1, copy_basis, 1),
            (-1, quant_left, 1), (0, psi_wide, 2), (1, quant_basis, 0), (0, vpsi_narrow, 3), (0, kin, 2),
            (0, scale_wide, 2), (0, kin, 3), (1, quant_basis, 1), (0, hpsi, 2), (0, psi_wide, 3), (0, hpsi, 3),
            (-1, quant_hpsi, 1), (0, scale_wide, 3), (0, quant_hpsi, 0), (0, weave_left),
        ]
        for r in range(GG + 1):
            for entry in round_steps:
                lag, step, args = entry[0], entry[1], entry[2:]
                if 0 <= r + lag < GG:
                    step(r + lag, *args)

        nc.scalar.activation(out=d_col[:], in_=d_raw[:], func=COPY)
        for h in range(NG):
            for pair in range(2):
                scale_a(h, pair)

        tiles = [(s, h) for s in range(len(SLABS)) for h in range(NG)]
        r_banks = [(s, h, b) for s, h in tiles for b in range(PACK * SLABS[s][1] // PASS)]
        last_slab = len(SLABS) - 1
        last_chunks = range(SLABS[last_slab][0] // CW, N // CW)
        late = [(j, c) for j in range(GG) for c in last_chunks]

        def finish_bank(s, h, b):
            finish_y(s, h, b)
            complete = slots(s, b).stop == PACK
            if s == 0:
                store_y(s, h, b, b + 1)
            elif complete:
                store_y(s, h, 0, PACK)
            if complete:
                round_y(s, h, (s, h) == tiles[-1])
            n = tiles.index((s, h))
            if b == 0 and n >= 2:
                quant_y(*tiles[n - 2])

        kin(*late[0])
        for n, r_bank in enumerate(r_banks):
            if n + 1 < len(late):
                kin(*late[n + 1])
            rayleigh(*r_bank)
            if n < len(late):
                hpsi(*late[n])
            if n > 0:
                finish_bank(*r_banks[n - 1])
            if n < len(late) and late[n][1] == last_chunks[-1]:
                quant_hpsi(late[n][0], last_slab)
        finish_bank(*r_banks[-1])
        for tile in tiles[-2:]:
            quant_y(*tile)
        store_scales(SLABS[0][1], N - SLABS[0][1], [nc.scalar, nc.sync])
